import numpy as np
import ml_dtypes


def mxq(x, axis, fmt="e4m3"):
    dtype, down = {"e4m3": (ml_dtypes.float8_e4m3fn, 7), "e5m2": (ml_dtypes.float8_e5m2, 14)}[fmt]
    v = np.moveaxis(np.asarray(x, np.float32).astype(ml_dtypes.bfloat16).astype(np.float64), axis, -1)
    blocks = v.reshape(v.shape[:-1] + (-1, 32))
    amax = np.abs(blocks).max(-1, keepdims=True)
    byte = np.maximum(np.where(amax > 0, np.frexp(amax)[1] - 1 + 127, 0) - down, 1)
    scale = np.exp2(byte - 127.0)
    codes = (blocks / scale).astype(np.float32).astype(dtype).astype(np.float64)
    return np.moveaxis((codes * scale).reshape(v.shape), -1, axis)


WIDE = False


def mx_kscale(k):
    if not WIDE:
        return np.ones(k)
    levels = np.array([24, -24, 12, -12, 0])
    if k % 512:
        return np.exp2(np.random.permutation(np.resize(levels, k // 32))).repeat(32)
    a = np.empty((k // 512, 16))
    for p in range(k // 512):
        a[p, :8] = np.random.permutation(np.resize(levels, 8))
        for g in range(8):
            far = levels[np.abs(levels - a[p, g]) >= 10]
            a[p, g + 8] = far[np.random.randint(len(far))]
    return np.exp2(a.ravel()).repeat(32)


def f64(x):
    return np.asarray(x).astype(np.float64)


def striped(idx):
    return np.tile(idx.reshape(-1, 16).T, (8, 1)).astype(np.uint16)


def unstriped(offs):
    return offs[:16].T.reshape(-1).astype(np.int64)


E2M1 = np.array([0.0, 0.5, 1.0, 1.5, 2.0, 3.0, 4.0, 6.0, -0.0, -0.5, -1.0, -1.5, -2.0, -3.0, -4.0, -6.0])


def pack_weight(w, fmt):
    k, n = w.shape
    w = f64(np.asarray(w, np.float32).astype(ml_dtypes.bfloat16)).reshape(k // 32, 32, n)
    amax = np.abs(w).max(1)
    if fmt == "e4m3":
        byte = np.frexp(amax)[1] - 1 + 127 - 7
    else:
        mant, ex = np.frexp(amax / 6.0)
        byte = np.where(mant > 0.5, ex, ex - 1) + 127
    byte = np.clip(np.where(amax > 0, byte, 1), 1, 254)
    scaled = (w * np.exp2(127.0 - byte)[:, None, :]).reshape(k, n).astype(np.float32)
    by_word = np.ascontiguousarray(scaled.reshape(k // 512, 128, 4, n).transpose(0, 1, 3, 2))
    if fmt == "e4m3":
        words = by_word.astype(ml_dtypes.float8_e4m3fn).view(np.uint8)
    else:
        c = by_word.astype(ml_dtypes.float4_e2m1fn).view(np.uint8) & 0xF
        words = (c[..., 0::2] | (c[..., 1::2] << 4)).reshape(k // 512, 128, 2 * n)
    return np.ascontiguousarray(words), np.ascontiguousarray(byte.astype(np.uint8).reshape(k // 512, 16, n))


def unpack_weight(words, scales, fmt):
    g, _, n = scales.shape
    words = np.ascontiguousarray(words).reshape(g, 128, n, -1)
    if fmt == "e4m3":
        vals = words.view(ml_dtypes.float8_e4m3fn).astype(np.float64)
    else:
        nib = np.empty((g, 128, n, 4), np.uint8)
        nib[..., 0::2] = words & 0xF
        nib[..., 1::2] = words >> 4
        vals = E2M1[nib]
    vals = vals * np.repeat(np.exp2(scales.astype(np.float64) - 127.0), 8, axis=1)[..., None]
    return vals.transpose(0, 1, 3, 2).reshape(g * 512, n)


def pack_table4(v):
    words, scales = pack_weight(v, "e2m1")
    g, t = words.shape[0] // 2, v.shape[1]
    return np.ascontiguousarray(words.reshape(g, 2, 128, t, 2).transpose(0, 2, 3, 1, 4).reshape(g, 128, t, 4)), scales


def unpack_table4(words, scales):
    g, _, t, _ = words.shape
    return unpack_weight(words.reshape(g, 128, t, 2, 2).transpose(0, 3, 1, 2, 4).reshape(2 * g, 128, 2 * t), scales, "e2m1")


K, L, N, T, J = 1024, 512, 512, 4096, 512


def setup_inputs():
    n = np.random.standard_normal
    s = mx_kscale(K)[:, None]
    s2 = mx_kscale(L)[:, None]
    p_tab = pack_table4(n((K, T)) * s)
    p_w = pack_weight(n((K, N)) / np.sqrt(K) / s, "e2m1")
    return {
        "tab_words": p_tab[0],
        "tab_scales": p_tab[1],
        "w_words": p_w[0],
        "w_scales": p_w[1],
        "x": (n((L, J)) * s2).astype(np.float32),
        "wx": (n((L, N)) / np.sqrt(L) / s2).astype(np.float32),
        "iw0": (np.random.uniform(0.1, 0.6, J)).astype(np.float32),
        "iw1": (np.random.uniform(0.1, 0.6, J)).astype(np.float32),
        "offs": striped(np.concatenate([np.random.permutation(T)[:J] for _ in range(2)])),
    }


def reference(tab_words, tab_scales, w_words, w_scales, x, wx, iw0, iw1, offs):
    idx = unstriped(offs).reshape(2, J)
    tab_ = unpack_table4(tab_words, tab_scales)[:, idx]
    w_ = unpack_weight(w_words, w_scales, "e2m1")
    a0 = w_.T @ tab_[:, 0]
    a1 = w_.T @ tab_[:, 1]
    x_ = mxq(f64(x), 0, "e4m3")
    wx_ = mxq(f64(wx), 0, "e4m3")
    ax = wx_.T @ x_
    return a0 * f64(iw0)[None, :] + a1 * f64(iw1)[None, :] + ax

@@ -1,0 +1,207 @@
+from contextlib import ExitStack
+
+import concourse.mybir as mybir
+from concourse.masks import make_identity
+
+K, L, N, T, J = 1024, 512, 512, 4096, 512
+FLOPS = 2 * (2 * K + L) * N * J
+
+F32 = mybir.dt.float32
+BF16 = mybir.dt.bfloat16
+I32 = mybir.dt.int32
+U32 = mybir.dt.uint32
+U16 = mybir.dt.uint16
+U8 = mybir.dt.uint8
+FP8X4 = mybir.dt.float8_e4m3fn_x4
+FP4X4 = mybir.dt.float4_e2m1fn_x4
+COPY = mybir.ActivationFunctionType.Copy
+MULT = mybir.AluOpType.mult
+ADD = mybir.AluOpType.add
+
+P = 128
+
+
+def tile_list_interp_none_kernel(
+    tc, tab_words, tab_scales, w_words, w_scales, x, wx, iw0, iw1, offs, out
+):
+    nc = tc.nc
+    with ExitStack() as ctx:
+        keep = ctx.enter_context(tc.tile_pool(name="keep", bufs=1))
+        psum = ctx.enter_context(tc.psum_pool(name="psum", bufs=1))
+
+        def sb(shape, dtype, name, tag=None):
+            return keep.tile(shape, dtype, name=name, tag=tag or name, align_bytes=64)
+
+        def bank(shape, index, name):
+            return psum.tile(shape, F32, name=name, tag="bank%d" % index)
+
+        offsets = keep.tile([P, 2 * J // 16], U16, name="offsets")
+        nc.sync.dma_start(offsets[:], offs)
+
+        w_planes = sb([P, 2 * N], U8, "w_planes")
+        nc.gpsimd.memset(w_planes[:].bitcast(I32), 0)
+        iw_rows = sb([P, P], F32, "iw_rows")
+        nc.gpsimd.memset(iw_rows[:], 0.0)
+        scale_table = sb([P, T], U8, "scale_table", tag="late")
+        nc.sync.dma_start(
+            scale_table[0:32, :].bitcast(I32), tab_scales.rearrange("a q t -> (a q) t").bitcast(I32)
+        )
+        nc.vector.memset(scale_table[32:64, :].bitcast(I32), 0)
+        nc.vector.memset(scale_table[64:128, :].bitcast(I32), 0)
+        planes = [sb([P, 2 * J], U8, "plane%d" % a) for a in range(2)]
+        for a in range(2):
+            nc.vector.memset(planes[a][:].bitcast(I32), 0)
+
+        w_both = sb([P, 2, 2 * N], U8, "w_both")
+        nc.sync.dma_start(w_both[:].bitcast(I32), w_words.rearrange("a p b -> p a b").bitcast(I32))
+        for r in range(4):
+            nc.sync.dma_start(
+                w_planes[r:P:32, :].bitcast(I32).rearrange("q (a n) -> q a n", a=2),
+                w_scales.bitcast(I32)[:, r:16:4, :].rearrange("a q n -> q a n"),
+            )
+        table = sb([P, T], I32, "table")
+        nc.sync.dma_start(table[:], tab_words[0].rearrange("p t b -> p (t b)").bitcast(I32))
+
+        nc.gpsimd.dma_start(iw_rows[0:4, :], iw0.rearrange("(c p) -> c p", p=P))
+        nc.gpsimd.dma_start(iw_rows[4:8, :], iw1.rearrange("(c p) -> c p", p=P))
+        ident = sb([P, P], F32, "ident")
+        make_identity(nc, ident[:])
+
+        picked_scales = sb([P, 2 * J], U8, "picked_scales", tag="later")
+        nc.vector.tensor_copy(picked_scales[:], scale_table[:].indirect(offsets[:]))
+        for a in range(2):
+            for r in range(4):
+                eng = nc.gpsimd if (a == 1 and r >= 2) else nc.scalar
+                eng.dma_start(
+                    planes[a][r:P:32, :].bitcast(I32),
+                    picked_scales[16 * a + r : 16 * a + 16 : 4, :].bitcast(I32),
+                )
+        wx_raw = sb([P, 4, N], F32, "wx_raw", tag="late")
+        nc.sync.dma_start(wx_raw[:], wx.rearrange("(p t) n -> p t n", t=4))
+        x_raw = sb([P, 4, J], F32, "x_raw", tag="later")
+        nc.sync.dma_start(x_raw[:], x.rearrange("(p t) n -> p t n", t=4))
+
+        iw_bank = bank([P, P], 7, "iw_bank")
+        nc.tensor.transpose(iw_bank[:], iw_rows[:], ident[:])
+        iw_cols = sb([P, 8], F32, "iw_cols")
+        nc.scalar.activation(iw_cols[:], iw_bank[:, 0:8], COPY)
+
+        parted = []
+        for g in range(2):
+            picked = sb([P, J], U32, "picked%d" % g)
+            nc.vector.tensor_copy(picked[:], table[:].bitcast(U32).indirect(offsets[:, 32 * g : 32 * g + 32]))
+            halves = picked[:].bitcast(U16).rearrange("p (j d) -> p d j", d=2)
+            codes = sb([P, 4 * J], U8, "parted%d" % g)
+            nc.vector.tensor_copy(codes[:].bitcast(U16).rearrange("p (d j) -> p d j", d=2), halves)
+            parted.append([codes[:, 0 : 2 * J], codes[:, 2 * J : 4 * J]])
+
+        def project(g, jt, acc):
+            for a in range(2):
+                nc.tensor.matmul_mx(
+                    out=acc[:],
+                    lhsT=parted[g][a][:, 2 * P * jt : 2 * P * (jt + 1)].bitcast(FP4X4),
+                    lhsT_scale=planes[a][:, g * J + P * jt : g * J + P * (jt + 1)],
+                    rhs=w_both[:, a, :].bitcast(FP4X4),
+                    rhs_scale=w_planes[:, a * N : (a + 1) * N],
+                    start=(a == 0),
+                    stop=(a == 1),
+                )
+
+        def interleave(eng_copy, raw, lo, hi, name):
+            grouped = sb([P, hi - lo, 4], BF16, name)
+            eng_copy(
+                grouped[:].rearrange("p (c i) t -> p c t i", i=4),
+                raw[:, :, lo:hi].rearrange("p t (c i) -> p c t i", i=4),
+            )
+            return grouped
+
+        def quantize(grouped, codes, scales, lo, hi):
+            nc.vector.quantize_mx(
+                out=codes[:, lo:hi].bitcast(FP8X4),
+                scales=scales[:, lo:hi],
+                in_=grouped[:].rearrange("p c t -> p (c t)"),
+            )
+
+        wx_codes = sb([P, N], U32, "wx_codes")
+        wx_scales = sb([P, N], U8, "wx_scales")
+        x_codes = sb([P, J], U32, "x_codes")
+        x_scales = sb([P, J], U8, "x_scales")
+
+        a0 = [bank([P, N], jt, "a0_%d" % jt) for jt in range(4)]
+        a1 = [bank([P, N], 4 + jt, "a1_%d" % jt) for jt in range(4)]
+        u = [sb([P, N], F32, "u%d" % jt) for jt in range(4)]
+        v = [sb([P, N], F32, "v%d" % jt) for jt in range(4)]
+        ax_sb = [sb([P, 4, 256], F32, "ax_sb%d" % h) for h in range(2)]
+        out_v = out.rearrange("(nt p) j -> p nt j", p=P)
+
+        def scale_first(jt):
+            nc.scalar.activation(u[jt][:], a0[jt][:], COPY, scale=iw_cols[:, jt : jt + 1])
+
+        def scale_second(jt):
+            nc.vector.scalar_tensor_tensor(
+                v[jt][:], a1[jt][:], iw_cols[:, 4 + jt : 5 + jt], u[jt][:], MULT, ADD
+            )
+
+        def skip(h):
+            for pair in range(2):
+                acc = bank([P, 2, 256], 2 * h + pair, "ax%d%d" % (h, pair))
+                for i in range(2):
+                    nt = 2 * pair + i
+                    nc.tensor.matmul_mx(
+                        out=acc[:, i, :],
+                        lhsT=wx_codes[:, P * nt : P * (nt + 1)].bitcast(FP8X4),
+                        lhsT_scale=wx_scales[:, P * nt : P * (nt + 1)],
+                        rhs=x_codes[:, 256 * h : 256 * (h + 1)].bitcast(FP8X4),
+                        rhs_scale=x_scales[:, 256 * h : 256 * (h + 1)],
+                        start=True,
+                        stop=True,
+                    )
+                nc.scalar.copy(ax_sb[h][:, 2 * pair : 2 * pair + 2, :], acc[:])
+
+        turned = {}
+
+        def turn(jt):
+            turned[jt] = bank([P, 4, P], 4 + jt, "turned%d" % jt)
+            for nt in range(4):
+                nc.tensor.transpose(turned[jt][:, nt, :], v[jt][:, P * nt : P * (nt + 1)], ident[:])
+
+        def finish(jt):
+            o = sb([P, 4, P], F32, "o%d" % jt)
+            lo = P * (jt % 2)
+            nc.vector.tensor_tensor(o[:], turned[jt][:], ax_sb[jt // 2][:, :, lo : lo + P], ADD)
+            nc.sync.dma_start(out_v[:, :, P * jt : P * (jt + 1)], o[:])
+
+        project(0, 0, a0[0])
+        wg0 = interleave(nc.scalar.copy, wx_raw, 0, 256, "wx_g0")
+        project(0, 1, a0[1])
+        scale_first(0)
+        quantize(wg0, wx_codes, wx_scales, 0, 256)
+        project(1, 0, a1[0])
+        scale_first(1)
+        scale_second(0)
+        project(0, 2, a0[2])
+        wg1 = interleave(nc.scalar.copy, wx_raw, 256, 512, "wx_g1")
+        xg0 = interleave(nc.vector.tensor_copy, x_raw, 0, 256, "x_g0")
+        project(1, 1, a1[1])
+        quantize(wg1, wx_codes, wx_scales, 256, 512)
+        quantize(xg0, x_codes, x_scales, 0, 256)
+        scale_first(2)
+        project(0, 3, a0[3])
+        scale_second(1)
+        xg1 = interleave(nc.scalar.copy, x_raw, 256, 512, "x_g1")
+        scale_first(3)
+        skip(0)
+        project(1, 2, a1[2])
+        turn(0)
+        turn(1)
+        quantize(xg1, x_codes, x_scales, 256, 512)
+        scale_second(2)
+        project(1, 3, a1[3])
+        finish(0)
+        skip(1)
+        scale_second(3)
+        finish(1)
+        turn(2)
+        turn(3)
+        finish(2)
+        finish(3)

@@ -1,7 +1,6 @@
 from contextlib import ExitStack
 
 import concourse.mybir as mybir
-from concourse.masks import make_identity
 
 K, L, N, T, J = 1024, 512, 512, 4096, 512
 FLOPS = 2 * (2 * K + L) * N * J
@@ -19,6 +18,12 @@ MULT = mybir.AluOpType.mult
 ADD = mybir.AluOpType.add
 
 P = 128
+PACK = 4
+QUAD = 32
+TILES = 4
+HALF = 256
+SHIFT = 16
+LIST_COLS = J // 16
 
 
 def tile_list_interp_none_kernel(
@@ -29,179 +34,199 @@ def tile_list_interp_none_kernel(
         keep = ctx.enter_context(tc.tile_pool(name="keep", bufs=1))
         psum = ctx.enter_context(tc.psum_pool(name="psum", bufs=1))
 
-        def sb(shape, dtype, name, tag=None):
-            return keep.tile(shape, dtype, name=name, tag=tag or name, align_bytes=64)
+        def sbuf(shape, dtype, name, slot=None):
+            return keep.tile(shape, dtype, name=name, tag=slot or name, align_bytes=64)
 
         def bank(shape, index, name):
             return psum.tile(shape, F32, name=name, tag="bank%d" % index)
 
-        offsets = keep.tile([P, 2 * J // 16], U16, name="offsets")
+        offsets = keep.tile([P, 2 * LIST_COLS], U16, name="offsets")
         nc.sync.dma_start(offsets[:], offs)
 
-        w_planes = sb([P, 2 * N], U8, "w_planes")
-        nc.gpsimd.memset(w_planes[:].bitcast(I32), 0)
-        iw_rows = sb([P, P], F32, "iw_rows")
-        nc.gpsimd.memset(iw_rows[:], 0.0)
-        scale_table = sb([P, T], U8, "scale_table", tag="late")
-        nc.sync.dma_start(
-            scale_table[0:32, :].bitcast(I32), tab_scales.rearrange("a q t -> (a q) t").bitcast(I32)
-        )
-        nc.vector.memset(scale_table[32:64, :].bitcast(I32), 0)
-        nc.vector.memset(scale_table[64:128, :].bitcast(I32), 0)
-        planes = [sb([P, 2 * J], U8, "plane%d" % a) for a in range(2)]
-        for a in range(2):
-            nc.vector.memset(planes[a][:].bitcast(I32), 0)
+        scale_table = sbuf([P, T], U8, "scale_table")
+        nc.gpsimd.memset(scale_table[:, 0 : T // 2].bitcast(I32), 0)
+        nc.vector.memset(scale_table[:, T // 2 : T].bitcast(I32), 0)
+        zeros = sbuf([P, P], F32, "zeros")
+        nc.gpsimd.memset(zeros[:], 0.0)
 
-        w_both = sb([P, 2, 2 * N], U8, "w_both")
-        nc.sync.dma_start(w_both[:].bitcast(I32), w_words.rearrange("a p b -> p a b").bitcast(I32))
+        iw_rows = sbuf([P, P], F32, "iw_rows")
+        nc.gpsimd.memset(iw_rows[:], 0.0)
+        nc.sync.dma_start(iw_rows[0:TILES, :], iw0.rearrange("(c p) -> c p", p=P))
+        nc.sync.dma_start(iw_rows[TILES : 2 * TILES, :], iw1.rearrange("(c p) -> c p", p=P))
         for r in range(4):
             nc.sync.dma_start(
-                w_planes[r:P:32, :].bitcast(I32).rearrange("q (a n) -> q a n", a=2),
-                w_scales.bitcast(I32)[:, r:16:4, :].rearrange("a q n -> q a n"),
+                scale_table[r:P:SHIFT, :].bitcast(I32),
+                tab_scales.bitcast(I32)[:, r:16:4, :].rearrange("a q t -> q a t"),
             )
-        table = sb([P, T], I32, "table")
+
+        ident = sbuf([P, P], F32, "ident")
+        nc.gpsimd.affine_select(
+            out=ident[:],
+            in_=zeros[:],
+            compare_op=mybir.AluOpType.not_equal,
+            fill=1.0,
+            base=0,
+            pattern=[[-1, P]],
+            channel_multiplier=1,
+        )
+        table = sbuf([P, T], I32, "table", slot="zeros")
         nc.sync.dma_start(table[:], tab_words[0].rearrange("p t b -> p (t b)").bitcast(I32))
 
-        nc.gpsimd.dma_start(iw_rows[0:4, :], iw0.rearrange("(c p) -> c p", p=P))
-        nc.gpsimd.dma_start(iw_rows[4:8, :], iw1.rearrange("(c p) -> c p", p=P))
-        ident = sb([P, P], F32, "ident")
-        make_identity(nc, ident[:])
-
-        picked_scales = sb([P, 2 * J], U8, "picked_scales", tag="later")
-        nc.vector.tensor_copy(picked_scales[:], scale_table[:].indirect(offsets[:]))
-        for a in range(2):
-            for r in range(4):
-                eng = nc.gpsimd if (a == 1 and r >= 2) else nc.scalar
-                eng.dma_start(
-                    planes[a][r:P:32, :].bitcast(I32),
-                    picked_scales[16 * a + r : 16 * a + 16 : 4, :].bitcast(I32),
-                )
-        wx_raw = sb([P, 4, N], F32, "wx_raw", tag="late")
-        nc.sync.dma_start(wx_raw[:], wx.rearrange("(p t) n -> p t n", t=4))
-        x_raw = sb([P, 4, J], F32, "x_raw", tag="later")
-        nc.sync.dma_start(x_raw[:], x.rearrange("(p t) n -> p t n", t=4))
+        w_planes = sbuf([P, 2 * N], U8, "w_planes")
+        nc.gpsimd.memset(w_planes[:].bitcast(I32), 0)
+        for r in range(4):
+            nc.sync.dma_start(
+                w_planes[r:P:QUAD, :].bitcast(I32).rearrange("q (a n) -> q a n", a=2),
+                w_scales.bitcast(I32)[:, r:16:4, :].rearrange("a q n -> q a n"),
+            )
 
         iw_bank = bank([P, P], 7, "iw_bank")
         nc.tensor.transpose(iw_bank[:], iw_rows[:], ident[:])
-        iw_cols = sb([P, 8], F32, "iw_cols")
-        nc.scalar.activation(iw_cols[:], iw_bank[:, 0:8], COPY)
+        iw_cols = sbuf([P, 2 * TILES], F32, "iw_cols")
+        nc.scalar.activation(iw_cols[:], iw_bank[:, 0 : 2 * TILES], COPY)
 
-        parted = []
+        w_codes = sbuf([P, 2, 2 * N], U8, "w_codes", slot="iw_rows")
+        nc.sync.dma_start(w_codes[:].bitcast(I32), w_words.rearrange("a p b -> p a b").bitcast(I32))
+
+        plane1 = sbuf([P, 2 * J], U8, "plane1")
+        nc.vector.memset(plane1[P - QUAD : P, :].bitcast(I32), 0)
+        plane0 = sbuf([P, 2 * J], U8, "plane0")
+        nc.vector.tensor_copy(plane0[:], scale_table[:].indirect(offsets[:]))
+        planes = [plane0, plane1]
+
+        raw = sbuf([P, 4 * PACK * HALF], F32, "raw", slot="scale_table")
+        pieces = [
+            raw[:, PACK * HALF * i : PACK * HALF * (i + 1)].rearrange("p (t c) -> p t c", t=PACK)
+            for i in range(4)
+        ]
+        wx_raw, x_raw = pieces[0:2], pieces[2:4]
+        wx_rows = wx.rearrange("(p t) n -> p t n", t=PACK)
+        x_rows = x.rearrange("(p t) j -> p t j", t=PACK)
+        nc.sync.dma_start(wx_raw[0], wx_rows[:, :, 0:HALF])
+        nc.sync.dma_start(plane1[0 : P - SHIFT, :].bitcast(I32), plane0[SHIFT:P, :].bitcast(I32))
+        nc.sync.dma_start(wx_raw[1], wx_rows[:, :, HALF : 2 * HALF])
+        for h in range(2):
+            nc.sync.dma_start(x_raw[h], x_rows[:, :, HALF * h : HALF * (h + 1)])
+
+        tab_codes = {}
         for g in range(2):
-            picked = sb([P, J], U32, "picked%d" % g)
-            nc.vector.tensor_copy(picked[:], table[:].bitcast(U32).indirect(offsets[:, 32 * g : 32 * g + 32]))
-            halves = picked[:].bitcast(U16).rearrange("p (j d) -> p d j", d=2)
-            codes = sb([P, 4 * J], U8, "parted%d" % g)
-            nc.vector.tensor_copy(codes[:].bitcast(U16).rearrange("p (d j) -> p d j", d=2), halves)
-            parted.append([codes[:, 0 : 2 * J], codes[:, 2 * J : 4 * J]])
+            picked = sbuf([P, J], U32, "picked%d" % g, slot="picked")
+            nc.vector.tensor_copy(
+                picked[:], table[:].bitcast(U32).indirect(offsets[:, LIST_COLS * g : LIST_COLS * (g + 1)])
+            )
+            by_pass = picked[:].bitcast(U16).rearrange("p (j a) -> p a j", a=2)
+            for lo, hi in ((0, 1), (1, TILES)):
+                width = P * (hi - lo)
+                parted = sbuf([P, 2 * 2 * width], U8, "parted%d%d" % (g, lo))
+                nc.vector.tensor_copy(
+                    parted[:].bitcast(U16).rearrange("p (a j) -> p a j", a=2), by_pass[:, :, P * lo : P * hi]
+                )
+                for jt in range(lo, hi):
+                    for a in range(2):
+                        first_byte = 2 * (a * width + P * (jt - lo))
+                        tab_codes[g, a, jt] = parted[:, first_byte : first_byte + 2 * P]
 
         def project(g, jt, acc):
-            for a in range(2):
+            for a in (1, 0):
                 nc.tensor.matmul_mx(
                     out=acc[:],
-                    lhsT=parted[g][a][:, 2 * P * jt : 2 * P * (jt + 1)].bitcast(FP4X4),
+                    lhsT=tab_codes[g, a, jt].bitcast(FP4X4),
                     lhsT_scale=planes[a][:, g * J + P * jt : g * J + P * (jt + 1)],
-                    rhs=w_both[:, a, :].bitcast(FP4X4),
+                    rhs=w_codes[:, a, :].bitcast(FP4X4),
                     rhs_scale=w_planes[:, a * N : (a + 1) * N],
-                    start=(a == 0),
-                    stop=(a == 1),
+                    start=(a == 1),
+                    stop=(a == 0),
                 )
 
-        def interleave(eng_copy, raw, lo, hi, name):
-            grouped = sb([P, hi - lo, 4], BF16, name)
-            eng_copy(
-                grouped[:].rearrange("p (c i) t -> p c t i", i=4),
-                raw[:, :, lo:hi].rearrange("p t (c i) -> p c t i", i=4),
+        def interleave(copy, rows, name):
+            grouped = sbuf([P, HALF, PACK], BF16, name)
+            copy(
+                grouped[:].rearrange("p (c i) t -> p c t i", i=2),
+                rows.rearrange("p t (c i) -> p c t i", i=2),
             )
             return grouped
 
-        def quantize(grouped, codes, scales, lo, hi):
+        def quantize(grouped, codes, scales, h):
             nc.vector.quantize_mx(
-                out=codes[:, lo:hi].bitcast(FP8X4),
-                scales=scales[:, lo:hi],
+                out=codes[:, HALF * h : HALF * (h + 1)].bitcast(FP8X4),
+                scales=scales[:, HALF * h : HALF * (h + 1)],
                 in_=grouped[:].rearrange("p c t -> p (c t)"),
             )
 
-        wx_codes = sb([P, N], U32, "wx_codes")
-        wx_scales = sb([P, N], U8, "wx_scales")
-        x_codes = sb([P, J], U32, "x_codes")
-        x_scales = sb([P, J], U8, "x_scales")
+        wx_codes = sbuf([P, N], U32, "wx_codes")
+        wx_scales = sbuf([P, N], U8, "wx_scales")
+        x_codes = sbuf([P, J], U32, "x_codes")
+        x_scales = sbuf([P, J], U8, "x_scales")
 
-        a0 = [bank([P, N], jt, "a0_%d" % jt) for jt in range(4)]
-        a1 = [bank([P, N], 4 + jt, "a1_%d" % jt) for jt in range(4)]
-        u = [sb([P, N], F32, "u%d" % jt) for jt in range(4)]
-        v = [sb([P, N], F32, "v%d" % jt) for jt in range(4)]
-        ax_sb = [sb([P, 4, 256], F32, "ax_sb%d" % h) for h in range(2)]
-        out_v = out.rearrange("(nt p) j -> p nt j", p=P)
+        a0 = [bank([P, N], jt, "a0_%d" % jt) for jt in range(TILES)]
+        a1 = [bank([P, N], TILES + jt, "a1_%d" % jt) for jt in range(TILES)]
+        first = {}
+        both = [sbuf([P, N], F32, "both%d" % jt) for jt in range(TILES)]
+        ax = [sbuf([P, TILES, P], F32, "ax%d" % jt) for jt in range(TILES)]
+        turned = {}
+        out_by_tile = out.rearrange("(nt p) j -> p nt j", p=P)
 
-        def scale_first(jt):
-            nc.scalar.activation(u[jt][:], a0[jt][:], COPY, scale=iw_cols[:, jt : jt + 1])
+        def weigh_first(jt):
+            first[jt] = sbuf([P, N], F32, "first%d" % jt)
+            nc.scalar.activation(first[jt][:], a0[jt][:], COPY, scale=iw_cols[:, jt : jt + 1])
 
-        def scale_second(jt):
+        def weigh_second(jt):
             nc.vector.scalar_tensor_tensor(
-                v[jt][:], a1[jt][:], iw_cols[:, 4 + jt : 5 + jt], u[jt][:], MULT, ADD
+                both[jt][:], a1[jt][:], iw_cols[:, TILES + jt : TILES + jt + 1], first[jt][:], MULT, ADD
             )
 
-        def skip(h):
-            for pair in range(2):
-                acc = bank([P, 2, 256], 2 * h + pair, "ax%d%d" % (h, pair))
-                for i in range(2):
-                    nt = 2 * pair + i
-                    nc.tensor.matmul_mx(
-                        out=acc[:, i, :],
-                        lhsT=wx_codes[:, P * nt : P * (nt + 1)].bitcast(FP8X4),
-                        lhsT_scale=wx_scales[:, P * nt : P * (nt + 1)],
-                        rhs=x_codes[:, 256 * h : 256 * (h + 1)].bitcast(FP8X4),
-                        rhs_scale=x_scales[:, 256 * h : 256 * (h + 1)],
-                        start=True,
-                        stop=True,
-                    )
-                nc.scalar.copy(ax_sb[h][:, 2 * pair : 2 * pair + 2, :], acc[:])
-
-        turned = {}
+        def skip(jt):
+            acc = bank([P, TILES, P], jt, "skip%d" % jt)
+            for nt in range(TILES):
+                nc.tensor.matmul_mx(
+                    out=acc[:, nt, :],
+                    lhsT=wx_codes[:, P * nt : P * (nt + 1)].bitcast(FP8X4),
+                    lhsT_scale=wx_scales[:, P * nt : P * (nt + 1)],
+                    rhs=x_codes[:, P * jt : P * (jt + 1)].bitcast(FP8X4),
+                    rhs_scale=x_scales[:, P * jt : P * (jt + 1)],
+                    start=True,
+                    stop=True,
+                )
+            nc.scalar.copy(ax[jt][:], acc[:])
 
         def turn(jt):
-            turned[jt] = bank([P, 4, P], 4 + jt, "turned%d" % jt)
-            for nt in range(4):
-                nc.tensor.transpose(turned[jt][:, nt, :], v[jt][:, P * nt : P * (nt + 1)], ident[:])
+            turned[jt] = bank([P, TILES, P], TILES + jt, "turned%d" % jt)
+            for nt in range(TILES):
+                nc.tensor.transpose(turned[jt][:, nt, :], both[jt][:, P * nt : P * (nt + 1)], ident[:])
 
         def finish(jt):
-            o = sb([P, 4, P], F32, "o%d" % jt)
-            lo = P * (jt % 2)
-            nc.vector.tensor_tensor(o[:], turned[jt][:], ax_sb[jt // 2][:, :, lo : lo + P], ADD)
-            nc.sync.dma_start(out_v[:, :, P * jt : P * (jt + 1)], o[:])
+            cuts = (0, TILES // 2, TILES) if jt == TILES - 1 else (0, TILES)
+            for lo, hi in zip(cuts, cuts[1:]):
+                result = sbuf([P, hi - lo, P], F32, "result%d%d" % (jt, lo))
+                nc.vector.tensor_tensor(result[:], turned[jt][:, lo:hi, :], ax[jt][:, lo:hi, :], ADD)
+                nc.sync.dma_start(out_by_tile[:, lo:hi, P * jt : P * (jt + 1)], result[:])
 
-        project(0, 0, a0[0])
-        wg0 = interleave(nc.scalar.copy, wx_raw, 0, 256, "wx_g0")
-        project(0, 1, a0[1])
-        scale_first(0)
-        quantize(wg0, wx_codes, wx_scales, 0, 256)
-        project(1, 0, a1[0])
-        scale_first(1)
-        scale_second(0)
-        project(0, 2, a0[2])
-        wg1 = interleave(nc.scalar.copy, wx_raw, 256, 512, "wx_g1")
-        xg0 = interleave(nc.vector.tensor_copy, x_raw, 0, 256, "x_g0")
-        project(1, 1, a1[1])
-        quantize(wg1, wx_codes, wx_scales, 256, 512)
-        quantize(xg0, x_codes, x_scales, 0, 256)
-        scale_first(2)
-        project(0, 3, a0[3])
-        scale_second(1)
-        xg1 = interleave(nc.scalar.copy, x_raw, 256, 512, "x_g1")
-        scale_first(3)
-        skip(0)
-        project(1, 2, a1[2])
-        turn(0)
-        turn(1)
-        quantize(xg1, x_codes, x_scales, 256, 512)
-        scale_second(2)
-        project(1, 3, a1[3])
-        finish(0)
-        skip(1)
-        scale_second(3)
-        finish(1)
-        turn(2)
-        turn(3)
-        finish(2)
-        finish(3)
+        for jt in range(TILES):
+            project(0, jt, a0[jt])
+        for jt in range(TILES):
+            project(1, jt, a1[jt])
+
+        wx_lo = interleave(nc.scalar.copy, wx_raw[0], "wx_lo")
+        weigh_first(0)
+        wx_hi = interleave(nc.scalar.copy, wx_raw[1], "wx_hi")
+        quantize(wx_lo, wx_codes, wx_scales, 0)
+        x_lo = interleave(nc.vector.tensor_copy, x_raw[0], "x_lo")
+        quantize(wx_hi, wx_codes, wx_scales, 1)
+        quantize(x_lo, x_codes, x_scales, 0)
+        weigh_second(0)
+        weigh_first(1)
+        weigh_second(1)
+        weigh_first(2)
+        x_hi = interleave(nc.scalar.copy, x_raw[1], "x_hi")
+        weigh_second(2)
+        quantize(x_hi, x_codes, x_scales, 1)
+        weigh_first(3)
+        weigh_second(3)
+
+        for pair in ((0, 1), (2, 3)):
+            for jt in pair:
+                skip(jt)
+            for jt in pair:
+                turn(jt)
+            for jt in pair:
+                finish(jt)

@@ -158,6 +158,18 @@ def tile_list_interp_none_kernel(
         x_codes = sbuf([P, J], U32, "x_codes")
         x_scales = sbuf([P, J], U8, "x_scales")
 
+        warm_up = bank([P, N], TILES - 1, "warm_up")
+        for a in range(2):
+            nc.tensor.matmul_mx(
+                out=warm_up[:],
+                lhsT=w_codes[:, a, 0 : 2 * P].bitcast(FP4X4),
+                lhsT_scale=w_planes[:, a * N : a * N + P],
+                rhs=w_codes[:, a, :].bitcast(FP4X4),
+                rhs_scale=w_planes[:, a * N : (a + 1) * N],
+                start=(a == 0),
+                stop=(a == 1),
+            )
+
         a0 = [bank([P, N], jt, "a0_%d" % jt) for jt in range(TILES)]
         a1 = [bank([P, N], TILES + jt, "a1_%d" % jt) for jt in range(TILES)]
         first = {}

@@ -22,7 +22,7 @@ PACK = 4
 QUAD = 32
 TILES = 4
 HALF = 256
-SHIFT = 16
+ROWS = 96
 LIST_COLS = J // 16
 
 
@@ -32,6 +32,7 @@ def tile_list_interp_none_kernel(
     nc = tc.nc
     with ExitStack() as ctx:
         keep = ctx.enter_context(tc.tile_pool(name="keep", bufs=1))
+        late = ctx.enter_context(tc.tile_pool(name="late", bufs=1))
         psum = ctx.enter_context(tc.psum_pool(name="psum", bufs=1))
 
         def sbuf(shape, dtype, name, slot=None):
@@ -43,22 +44,33 @@ def tile_list_interp_none_kernel(
         offsets = keep.tile([P, 2 * LIST_COLS], U16, name="offsets")
         nc.sync.dma_start(offsets[:], offs)
 
-        scale_table = sbuf([P, T], U8, "scale_table")
-        nc.gpsimd.memset(scale_table[:, 0 : T // 2].bitcast(I32), 0)
-        nc.vector.memset(scale_table[:, T // 2 : T].bitcast(I32), 0)
-        zeros = sbuf([P, P], F32, "zeros")
-        nc.gpsimd.memset(zeros[:], 0.0)
+        scale_table = late.tile([P, T], U8, name="scale_table", offset=0, align_bytes=64)
+        for a in range(2):
+            nc.scalar.dma_start(scale_table[ROWS + a : P : 2, :].bitcast(I32), tab_scales.bitcast(I32)[a])
+
+        w_planes = sbuf([P, 2 * N], U8, "w_planes")
+        nc.vector.memset(w_planes[:, 0:N].bitcast(I32), 0)
+        nc.gpsimd.memset(w_planes[:, N : 2 * N].bitcast(I32), 0)
+        for r, queue in enumerate((nc.sync, nc.scalar, nc.sync, nc.scalar)):
+            queue.dma_start(
+                w_planes[r:P:QUAD, :].bitcast(I32).rearrange("q (a n) -> q a n", a=2),
+                w_scales.bitcast(I32)[:, r:16:4, :].rearrange("a q n -> q a n"),
+            )
+
+        table = sbuf([P, T], I32, "table")
+        nc.scalar.dma_start(table[:], tab_words[0].rearrange("p t b -> p (t b)").bitcast(I32))
+
+        nc.vector.memset(scale_table[0:ROWS, :].bitcast(I32), 0)
+        planes = sbuf([P, 2, 2 * J], U8, "planes")
+        nc.vector.memset(planes[:].bitcast(I32), 0)
 
         iw_rows = sbuf([P, P], F32, "iw_rows")
         nc.gpsimd.memset(iw_rows[:], 0.0)
-        nc.sync.dma_start(iw_rows[0:TILES, :], iw0.rearrange("(c p) -> c p", p=P))
-        nc.sync.dma_start(iw_rows[TILES : 2 * TILES, :], iw1.rearrange("(c p) -> c p", p=P))
-        for r in range(4):
-            nc.sync.dma_start(
-                scale_table[r:P:SHIFT, :].bitcast(I32),
-                tab_scales.bitcast(I32)[:, r:16:4, :].rearrange("a q t -> q a t"),
-            )
+        nc.gpsimd.dma_start(iw_rows[0:TILES, :], iw0.rearrange("(c p) -> c p", p=P))
+        nc.gpsimd.dma_start(iw_rows[TILES : 2 * TILES, :], iw1.rearrange("(c p) -> c p", p=P))
 
+        zeros = sbuf([P, P], F32, "zeros")
+        nc.gpsimd.memset(zeros[:], 0.0)
         ident = sbuf([P, P], F32, "ident")
         nc.gpsimd.affine_select(
             out=ident[:],
@@ -69,79 +81,73 @@ def tile_list_interp_none_kernel(
             pattern=[[-1, P]],
             channel_multiplier=1,
         )
-        table = sbuf([P, T], I32, "table", slot="zeros")
-        nc.sync.dma_start(table[:], tab_words[0].rearrange("p t b -> p (t b)").bitcast(I32))
 
-        w_planes = sbuf([P, 2 * N], U8, "w_planes")
-        nc.gpsimd.memset(w_planes[:].bitcast(I32), 0)
-        for r in range(4):
+        picked_scales = sbuf([P, 2 * J], U8, "picked_scales")
+        nc.vector.tensor_copy(picked_scales[:], scale_table[:].indirect(offsets[:]))
+
+        w_codes = late.tile([P, 2, 2 * N], U8, name="w_codes", offset=0, align_bytes=64)
+        nc.sync.dma_start(w_codes[:].bitcast(I32), w_words.rearrange("a p b -> p a b").bitcast(I32))
+        for q in range(4):
             nc.sync.dma_start(
-                w_planes[r:P:QUAD, :].bitcast(I32).rearrange("q (a n) -> q a n", a=2),
-                w_scales.bitcast(I32)[:, r:16:4, :].rearrange("a q n -> q a n"),
+                planes[QUAD * q : QUAD * q + 4, :, :].bitcast(I32),
+                picked_scales[ROWS + 8 * q : ROWS + 8 * q + 8, :].bitcast(I32),
             )
 
-        iw_bank = bank([P, P], 7, "iw_bank")
-        nc.tensor.transpose(iw_bank[:], iw_rows[:], ident[:])
-        iw_cols = sbuf([P, 2 * TILES], F32, "iw_cols")
-        nc.scalar.activation(iw_cols[:], iw_bank[:, 0 : 2 * TILES], COPY)
-
-        w_codes = sbuf([P, 2, 2 * N], U8, "w_codes", slot="iw_rows")
-        nc.sync.dma_start(w_codes[:].bitcast(I32), w_words.rearrange("a p b -> p a b").bitcast(I32))
-
-        plane1 = sbuf([P, 2 * J], U8, "plane1")
-        nc.vector.memset(plane1[P - QUAD : P, :].bitcast(I32), 0)
-        plane0 = sbuf([P, 2 * J], U8, "plane0")
-        nc.vector.tensor_copy(plane0[:], scale_table[:].indirect(offsets[:]))
-        planes = [plane0, plane1]
-
-        raw = sbuf([P, 4 * PACK * HALF], F32, "raw", slot="scale_table")
-        pieces = [
-            raw[:, PACK * HALF * i : PACK * HALF * (i + 1)].rearrange("p (t c) -> p t c", t=PACK)
-            for i in range(4)
-        ]
-        wx_raw, x_raw = pieces[0:2], pieces[2:4]
         wx_rows = wx.rearrange("(p t) n -> p t n", t=PACK)
         x_rows = x.rearrange("(p t) j -> p t j", t=PACK)
-        nc.sync.dma_start(wx_raw[0], wx_rows[:, :, 0:HALF])
-        nc.sync.dma_start(plane1[0 : P - SHIFT, :].bitcast(I32), plane0[SHIFT:P, :].bitcast(I32))
-        nc.sync.dma_start(wx_raw[1], wx_rows[:, :, HALF : 2 * HALF])
+        raw = late.tile([P, 4 * PACK * HALF], F32, name="raw", offset=4 * N, align_bytes=64)
+        pieces = [
+            raw[:, PACK * HALF * i : PACK * HALF * (i + 1)].rearrange("p (t c) -> p t c", t=PACK) for i in range(4)
+        ]
+        wx_raw, x_raw = pieces[0:2], pieces[2:4]
+        for h in range(2):
+            nc.sync.dma_start(wx_raw[h], wx_rows[:, :, HALF * h : HALF * (h + 1)])
         for h in range(2):
             nc.sync.dma_start(x_raw[h], x_rows[:, :, HALF * h : HALF * (h + 1)])
 
+        picked = sbuf([P, J + HALF], U32, "picked")
         tab_codes = {}
-        for g in range(2):
-            picked = sbuf([P, J], U32, "picked%d" % g, slot="picked")
+
+        def gather(g):
+            lo = HALF * (1 - g)
             nc.vector.tensor_copy(
-                picked[:], table[:].bitcast(U32).indirect(offsets[:, LIST_COLS * g : LIST_COLS * (g + 1)])
+                picked[:, lo : lo + J], table[:].bitcast(U32).indirect(offsets[:, LIST_COLS * g : LIST_COLS * (g + 1)])
             )
-            by_pass = picked[:].bitcast(U16).rearrange("p (j a) -> p a j", a=2)
-            for lo, hi in ((0, 1), (1, TILES)):
-                width = P * (hi - lo)
-                parted = sbuf([P, 2 * 2 * width], U8, "parted%d%d" % (g, lo))
-                nc.vector.tensor_copy(
-                    parted[:].bitcast(U16).rearrange("p (a j) -> p a j", a=2), by_pass[:, :, P * lo : P * hi]
-                )
-                for jt in range(lo, hi):
-                    for a in range(2):
-                        first_byte = 2 * (a * width + P * (jt - lo))
-                        tab_codes[g, a, jt] = parted[:, first_byte : first_byte + 2 * P]
+
+        def part(g, h):
+            lo = HALF * (1 - g + h)
+            parted = sbuf([P, 2 * 2 * HALF], U8, "parted%d%d" % (g, h))
+            nc.vector.tensor_copy(
+                parted[:].bitcast(U16).rearrange("p (a j) -> p a j", a=2),
+                picked[:, lo : lo + HALF].bitcast(U16).rearrange("p (j a) -> p a j", a=2),
+            )
+            for i in range(2):
+                for a in range(2):
+                    first_byte = 2 * (a * HALF + P * i)
+                    tab_codes[g, a, 2 * h + i] = parted[:, first_byte : first_byte + 2 * P]
+
+        gather(0)
+        part(0, 0)
+        gather(1)
+        part(0, 1)
+        part(1, 0)
+        part(1, 1)
 
         def project(g, jt, acc):
             for a in (1, 0):
                 nc.tensor.matmul_mx(
                     out=acc[:],
                     lhsT=tab_codes[g, a, jt].bitcast(FP4X4),
-                    lhsT_scale=planes[a][:, g * J + P * jt : g * J + P * (jt + 1)],
+                    lhsT_scale=planes[:, a, g * J + P * jt : g * J + P * (jt + 1)],
                     rhs=w_codes[:, a, :].bitcast(FP4X4),
                     rhs_scale=w_planes[:, a * N : (a + 1) * N],
                     start=(a == 1),
                     stop=(a == 0),
                 )
 
-        def interleave(copy, rows, name):
-            grouped = sbuf([P, HALF, PACK], BF16, name)
+        def interleave(copy, rows, grouped):
             copy(
-                grouped[:].rearrange("p (c i) t -> p c t i", i=2),
+                grouped.rearrange("p (c i) t -> p c t i", i=2),
                 rows.rearrange("p t (c i) -> p c t i", i=2),
             )
             return grouped
@@ -150,7 +156,7 @@ def tile_list_interp_none_kernel(
             nc.vector.quantize_mx(
                 out=codes[:, HALF * h : HALF * (h + 1)].bitcast(FP8X4),
                 scales=scales[:, HALF * h : HALF * (h + 1)],
-                in_=grouped[:].rearrange("p c t -> p (c t)"),
+                in_=grouped.rearrange("p c t -> p (c t)"),
             )
 
         wx_codes = sbuf([P, N], U32, "wx_codes")
@@ -158,87 +164,87 @@ def tile_list_interp_none_kernel(
         x_codes = sbuf([P, J], U32, "x_codes")
         x_scales = sbuf([P, J], U8, "x_scales")
 
-        warm_up = bank([P, N], TILES - 1, "warm_up")
+        warm_up = bank([P, N], 7, "warm_up")
+        table_bytes = table[:].bitcast(U8)
         for a in range(2):
             nc.tensor.matmul_mx(
                 out=warm_up[:],
-                lhsT=w_codes[:, a, 0 : 2 * P].bitcast(FP4X4),
-                lhsT_scale=w_planes[:, a * N : a * N + P],
-                rhs=w_codes[:, a, :].bitcast(FP4X4),
-                rhs_scale=w_planes[:, a * N : (a + 1) * N],
+                lhsT=table_bytes[:, 0 : 2 * P].bitcast(FP4X4),
+                lhsT_scale=w_planes[:, 0:P],
+                rhs=table_bytes[:, 0 : 2 * N].bitcast(FP4X4),
+                rhs_scale=w_planes[:, 0:N],
                 start=(a == 0),
                 stop=(a == 1),
             )
+
+        iw_bank = bank([P, P], 7, "iw_bank")
+        nc.tensor.transpose(iw_bank[:], iw_rows[:], ident[:])
+        iw_cols = [sbuf([P, TILES], F32, "iw_cols%d" % g) for g in range(2)]
+        for g in range(2):
+            nc.scalar.activation(iw_cols[g][:], iw_bank[:, TILES * g : TILES * (g + 1)], COPY)
 
         a0 = [bank([P, N], jt, "a0_%d" % jt) for jt in range(TILES)]
         a1 = [bank([P, N], TILES + jt, "a1_%d" % jt) for jt in range(TILES)]
         first = {}
         both = [sbuf([P, N], F32, "both%d" % jt) for jt in range(TILES)]
-        ax = [sbuf([P, TILES, P], F32, "ax%d" % jt) for jt in range(TILES)]
-        turned = {}
         out_by_tile = out.rearrange("(nt p) j -> p nt j", p=P)
 
         def weigh_first(jt):
             first[jt] = sbuf([P, N], F32, "first%d" % jt)
-            nc.scalar.activation(first[jt][:], a0[jt][:], COPY, scale=iw_cols[:, jt : jt + 1])
+            nc.scalar.activation(first[jt][:], a0[jt][:], COPY, scale=iw_cols[0][:, jt : jt + 1])
 
-        def weigh_second(jt):
+        def weigh_second(jt, lo=0, hi=N):
             nc.vector.scalar_tensor_tensor(
-                both[jt][:], a1[jt][:], iw_cols[:, TILES + jt : TILES + jt + 1], first[jt][:], MULT, ADD
+                both[jt][:, lo:hi], a1[jt][:, lo:hi], iw_cols[1][:, jt : jt + 1], first[jt][:, lo:hi], MULT, ADD
             )
 
-        def skip(jt):
-            acc = bank([P, TILES, P], jt, "skip%d" % jt)
-            for nt in range(TILES):
-                nc.tensor.matmul_mx(
-                    out=acc[:, nt, :],
-                    lhsT=wx_codes[:, P * nt : P * (nt + 1)].bitcast(FP8X4),
-                    lhsT_scale=wx_scales[:, P * nt : P * (nt + 1)],
-                    rhs=x_codes[:, P * jt : P * (jt + 1)].bitcast(FP8X4),
-                    rhs_scale=x_scales[:, P * jt : P * (jt + 1)],
-                    start=True,
-                    stop=True,
-                )
-            nc.scalar.copy(ax[jt][:], acc[:])
-
-        def turn(jt):
-            turned[jt] = bank([P, TILES, P], TILES + jt, "turned%d" % jt)
-            for nt in range(TILES):
-                nc.tensor.transpose(turned[jt][:, nt, :], both[jt][:, P * nt : P * (nt + 1)], ident[:])
-
-        def finish(jt):
-            cuts = (0, TILES // 2, TILES) if jt == TILES - 1 else (0, TILES)
-            for lo, hi in zip(cuts, cuts[1:]):
-                result = sbuf([P, hi - lo, P], F32, "result%d%d" % (jt, lo))
-                nc.vector.tensor_tensor(result[:], turned[jt][:, lo:hi, :], ax[jt][:, lo:hi, :], ADD)
-                nc.sync.dma_start(out_by_tile[:, lo:hi, P * jt : P * (jt + 1)], result[:])
+        def finish(h):
+            turned = [bank([P, 2, HALF], 2 * h + m, "turned%d%d" % (h, m)) for m in range(2)]
+            for jt in (2 * h, 2 * h + 1):
+                for nt in range(TILES):
+                    nc.tensor.transpose(
+                        turned[nt // 2][:, nt % 2, P * (jt % 2) : P * (jt % 2 + 1)],
+                        both[jt][:, P * nt : P * (nt + 1)],
+                        ident[:],
+                    )
+            for m in range(2):
+                ax = bank([P, 2, HALF], TILES + 2 * h + m, "ax%d%d" % (h, m))
+                for i in range(2):
+                    nt = 2 * m + i
+                    nc.tensor.matmul_mx(
+                        out=ax[:, i, :],
+                        lhsT=wx_codes[:, P * nt : P * (nt + 1)].bitcast(FP8X4),
+                        lhsT_scale=wx_scales[:, P * nt : P * (nt + 1)],
+                        rhs=x_codes[:, HALF * h : HALF * (h + 1)].bitcast(FP8X4),
+                        rhs_scale=x_scales[:, HALF * h : HALF * (h + 1)],
+                        start=True,
+                        stop=True,
+                    )
+                looked_up = sbuf([P, 2, HALF], F32, "looked_up%d%d" % (h, m))
+                nc.scalar.copy(looked_up[:], turned[m][:])
+                result = sbuf([P, 2, HALF], F32, "result%d%d" % (h, m))
+                nc.vector.tensor_tensor(result[:], ax[:], looked_up[:], ADD)
+                nc.sync.dma_start(out_by_tile[:, 2 * m : 2 * m + 2, HALF * h : HALF * (h + 1)], result[:])
 
         for jt in range(TILES):
             project(0, jt, a0[jt])
         for jt in range(TILES):
             project(1, jt, a1[jt])
 
-        wx_lo = interleave(nc.scalar.copy, wx_raw[0], "wx_lo")
-        weigh_first(0)
-        wx_hi = interleave(nc.scalar.copy, wx_raw[1], "wx_hi")
+        wx_grouped = [sbuf([P, HALF, PACK], BF16, "wx_grouped%d" % h) for h in range(2)]
+        wx_lo = interleave(nc.scalar.copy, wx_raw[0], wx_grouped[0][:])
+        for jt in range(TILES):
+            weigh_first(jt)
+        wx_hi = interleave(nc.vector.tensor_copy, wx_raw[1], wx_grouped[1][:])
         quantize(wx_lo, wx_codes, wx_scales, 0)
-        x_lo = interleave(nc.vector.tensor_copy, x_raw[0], "x_lo")
         quantize(wx_hi, wx_codes, wx_scales, 1)
-        quantize(x_lo, x_codes, x_scales, 0)
-        weigh_second(0)
-        weigh_first(1)
-        weigh_second(1)
-        weigh_first(2)
-        x_hi = interleave(nc.scalar.copy, x_raw[1], "x_hi")
-        weigh_second(2)
-        quantize(x_hi, x_codes, x_scales, 1)
-        weigh_first(3)
-        weigh_second(3)
 
-        for pair in ((0, 1), (2, 3)):
-            for jt in pair:
-                skip(jt)
-            for jt in pair:
-                turn(jt)
-            for jt in pair:
-                finish(jt)
+        x_grouped = sbuf([P, 2 * HALF * PACK], BF16, "x_grouped", slot="iw_cols0")
+        for h in range(2):
+            grouped = x_grouped[:, HALF * PACK * h : HALF * PACK * (h + 1)].rearrange("p (c t) -> p c t", t=PACK)
+            interleave(nc.scalar.copy, x_raw[h], grouped)
+            weigh_second(2 * h)
+            weigh_second(2 * h + 1)
+            quantize(grouped, x_codes, x_scales, h)
+        for h in range(2):
+            finish(h)

@@ -128,8 +128,8 @@ def tile_list_interp_none_kernel(
 
         gather(0)
         part(0, 0)
-        gather(1)
         part(0, 1)
+        gather(1)
         part(1, 0)
         part(1, 1)
 
@@ -164,7 +164,7 @@ def tile_list_interp_none_kernel(
         x_codes = sbuf([P, J], U32, "x_codes")
         x_scales = sbuf([P, J], U8, "x_scales")
 
-        warm_up = bank([P, N], 7, "warm_up")
+        warm_up = bank([P, N], 6, "warm_up")
         table_bytes = table[:].bitcast(U8)
         for a in range(2):
             nc.tensor.matmul_mx(
@@ -222,9 +222,11 @@ def tile_list_interp_none_kernel(
                     )
                 looked_up = sbuf([P, 2, HALF], F32, "looked_up%d%d" % (h, m))
                 nc.scalar.copy(looked_up[:], turned[m][:])
-                result = sbuf([P, 2, HALF], F32, "result%d%d" % (h, m))
-                nc.vector.tensor_tensor(result[:], ax[:], looked_up[:], ADD)
-                nc.sync.dma_start(out_by_tile[:, 2 * m : 2 * m + 2, HALF * h : HALF * (h + 1)], result[:])
+                cuts = (0, 1, 2) if (h, m) == (1, 1) else (0, 2)
+                for lo, hi in zip(cuts, cuts[1:]):
+                    result = sbuf([P, hi - lo, HALF], F32, "result%d%d%d" % (h, m, lo))
+                    nc.vector.tensor_tensor(result[:], ax[:, lo:hi, :], looked_up[:, lo:hi, :], ADD)
+                    nc.sync.dma_start(out_by_tile[:, 2 * m + lo : 2 * m + hi, HALF * h : HALF * (h + 1)], result[:])
 
         for jt in range(TILES):
             project(0, jt, a0[jt])

@@ -96,14 +96,14 @@ def tile_list_interp_none_kernel(
         wx_rows = wx.rearrange("(p t) n -> p t n", t=PACK)
         x_rows = x.rearrange("(p t) j -> p t j", t=PACK)
         raw = late.tile([P, 4 * PACK * HALF], F32, name="raw", offset=4 * N, align_bytes=64)
-        pieces = [
-            raw[:, PACK * HALF * i : PACK * HALF * (i + 1)].rearrange("p (t c) -> p t c", t=PACK) for i in range(4)
+        wx_raw = [
+            raw[:, PACK * HALF * h : PACK * HALF * (h + 1)].rearrange("p (t c) -> p t c", t=PACK) for h in range(2)
         ]
-        wx_raw, x_raw = pieces[0:2], pieces[2:4]
         for h in range(2):
             nc.sync.dma_start(wx_raw[h], wx_rows[:, :, HALF * h : HALF * (h + 1)])
-        for h in range(2):
-            nc.sync.dma_start(x_raw[h], x_rows[:, :, HALF * h : HALF * (h + 1)])
+        x_all = raw[:, PACK * N : PACK * (N + J)].rearrange("p (t c) -> p t c", t=PACK)
+        nc.sync.dma_start(x_all, x_rows)
+        x_raw = [x_all[:, :, HALF * h : HALF * (h + 1)] for h in range(2)]
 
         picked = sbuf([P, J + HALF], U32, "picked")
         tab_codes = {}
@@ -147,8 +147,8 @@ def tile_list_interp_none_kernel(
 
         def interleave(copy, rows, grouped):
             copy(
-                grouped.rearrange("p (c i) t -> p c t i", i=2),
-                rows.rearrange("p t (c i) -> p c t i", i=2),
+                grouped.rearrange("p (c i) t -> p c t i", i=PACK),
+                rows.rearrange("p t (c i) -> p c t i", i=PACK),
             )
             return grouped
 

@@ -45,8 +45,11 @@ def tile_list_interp_none_kernel(
         nc.sync.dma_start(offsets[:], offs)
 
         scale_table = late.tile([P, T], U8, name="scale_table", offset=0, align_bytes=64)
-        for a in range(2):
-            nc.scalar.dma_start(scale_table[ROWS + a : P : 2, :].bitcast(I32), tab_scales.bitcast(I32)[a])
+        nc.scalar.dma_start(scale_table[ROWS:P, :].bitcast(I32), tab_scales.bitcast(I32).rearrange("a i t -> i a t"))
+
+        table = sbuf([P, T], I32, "table")
+        table_words = tab_words[0].rearrange("p t b -> p (t b)").bitcast(I32)
+        nc.scalar.dma_start(table[:, 0 : T // 2], table_words[:, 0 : T // 2])
 
         w_planes = sbuf([P, 2 * N], U8, "w_planes")
         nc.vector.memset(w_planes[:, 0:N].bitcast(I32), 0)
@@ -57,8 +60,7 @@ def tile_list_interp_none_kernel(
                 w_scales.bitcast(I32)[:, r:16:4, :].rearrange("a q n -> q a n"),
             )
 
-        table = sbuf([P, T], I32, "table")
-        nc.scalar.dma_start(table[:], tab_words[0].rearrange("p t b -> p (t b)").bitcast(I32))
+        nc.scalar.dma_start(table[:, T // 2 : T], table_words[:, T // 2 : T])
 
         nc.vector.memset(scale_table[0:ROWS, :].bitcast(I32), 0)
         planes = sbuf([P, 2, 2 * J], U8, "planes")
@@ -165,7 +167,7 @@ def tile_list_interp_none_kernel(
         x_scales = sbuf([P, J], U8, "x_scales")
 
         warm_up = bank([P, N], 6, "warm_up")
-        table_bytes = table[:].bitcast(U8)
+        table_bytes = table[:, T // 2 : T].bitcast(U8)
         for a in range(2):
             nc.tensor.matmul_mx(
                 out=warm_up[:],
@@ -186,7 +188,7 @@ def tile_list_interp_none_kernel(
         a0 = [bank([P, N], jt, "a0_%d" % jt) for jt in range(TILES)]
         a1 = [bank([P, N], TILES + jt, "a1_%d" % jt) for jt in range(TILES)]
         first = {}
-        both = [sbuf([P, N], F32, "both%d" % jt) for jt in range(TILES)]
+        both = [sbuf([P, N], F32, "both%d" % jt) for jt in range(TILES - 1)]
         out_by_tile = out.rearrange("(nt p) j -> p nt j", p=P)
 
         def weigh_first(jt):
@@ -220,12 +222,12 @@ def tile_list_interp_none_kernel(
                         start=True,
                         stop=True,
                     )
-                looked_up = sbuf([P, 2, HALF], F32, "looked_up%d%d" % (h, m))
-                nc.scalar.copy(looked_up[:], turned[m][:])
                 cuts = (0, 1, 2) if (h, m) == (1, 1) else (0, 2)
                 for lo, hi in zip(cuts, cuts[1:]):
+                    looked_up = sbuf([P, hi - lo, HALF], F32, "looked_up%d%d%d" % (h, m, lo))
+                    nc.scalar.copy(looked_up[:], turned[m][:, lo:hi, :])
                     result = sbuf([P, hi - lo, HALF], F32, "result%d%d%d" % (h, m, lo))
-                    nc.vector.tensor_tensor(result[:], ax[:, lo:hi, :], looked_up[:, lo:hi, :], ADD)
+                    nc.vector.tensor_tensor(result[:], ax[:, lo:hi, :], looked_up[:], ADD)
                     nc.sync.dma_start(out_by_tile[:, 2 * m + lo : 2 * m + hi, HALF * h : HALF * (h + 1)], result[:])
 
         for jt in range(TILES):
@@ -242,6 +244,7 @@ def tile_list_interp_none_kernel(
         quantize(wx_hi, wx_codes, wx_scales, 1)
 
         x_grouped = sbuf([P, 2 * HALF * PACK], BF16, "x_grouped", slot="iw_cols0")
+        both.append(x_grouped[:, 0 : HALF * PACK].bitcast(F32))
         for h in range(2):
             grouped = x_grouped[:, HALF * PACK * h : HALF * PACK * (h + 1)].rearrange("p (c t) -> p c t", t=PACK)
             interleave(nc.scalar.copy, x_raw[h], grouped)

@@ -22,7 +22,9 @@ PACK = 4
 QUAD = 32
 TILES = 4
 HALF = 256
-ROWS = 96
+SCALE_ROWS = 96
+RAW = 4 * PACK * HALF
+ALIGN = 64
 LIST_COLS = J // 16
 
 
@@ -32,11 +34,11 @@ def tile_list_interp_none_kernel(
     nc = tc.nc
     with ExitStack() as ctx:
         keep = ctx.enter_context(tc.tile_pool(name="keep", bufs=1))
-        late = ctx.enter_context(tc.tile_pool(name="late", bufs=1))
+        placed = ctx.enter_context(tc.tile_pool(name="placed", bufs=1))
         psum = ctx.enter_context(tc.psum_pool(name="psum", bufs=1))
 
         def sbuf(shape, dtype, name, slot=None):
-            return keep.tile(shape, dtype, name=name, tag=slot or name, align_bytes=64)
+            return keep.tile(shape, dtype, name=name, tag=slot or name, align_bytes=ALIGN)
 
         def bank(shape, index, name):
             return psum.tile(shape, F32, name=name, tag="bank%d" % index)
@@ -44,8 +46,10 @@ def tile_list_interp_none_kernel(
         offsets = keep.tile([P, 2 * LIST_COLS], U16, name="offsets")
         nc.sync.dma_start(offsets[:], offs)
 
-        scale_table = late.tile([P, T], U8, name="scale_table", offset=0, align_bytes=64)
-        nc.scalar.dma_start(scale_table[ROWS:P, :].bitcast(I32), tab_scales.bitcast(I32).rearrange("a i t -> i a t"))
+        scale_table = placed.tile([P, T], U8, name="scale_table", offset=RAW - ALIGN, align_bytes=ALIGN)
+        nc.scalar.dma_start(
+            scale_table[SCALE_ROWS:P, :].bitcast(I32), tab_scales.bitcast(I32).rearrange("a q t -> q a t")
+        )
 
         table = sbuf([P, T], I32, "table")
         table_words = tab_words[0].rearrange("p t b -> p (t b)").bitcast(I32)
@@ -62,7 +66,7 @@ def tile_list_interp_none_kernel(
 
         nc.scalar.dma_start(table[:, T // 2 : T], table_words[:, T // 2 : T])
 
-        nc.vector.memset(scale_table[0:ROWS, :].bitcast(I32), 0)
+        nc.vector.memset(scale_table[0:SCALE_ROWS, :].bitcast(I32), 0)
         planes = sbuf([P, 2, 2 * J], U8, "planes")
         nc.vector.memset(planes[:].bitcast(I32), 0)
 
@@ -87,24 +91,24 @@ def tile_list_interp_none_kernel(
         picked_scales = sbuf([P, 2 * J], U8, "picked_scales")
         nc.vector.tensor_copy(picked_scales[:], scale_table[:].indirect(offsets[:]))
 
-        w_codes = late.tile([P, 2, 2 * N], U8, name="w_codes", offset=0, align_bytes=64)
+        w_codes = placed.tile([P, 2, 2 * N], U8, name="w_codes", offset=RAW, align_bytes=ALIGN)
         nc.sync.dma_start(w_codes[:].bitcast(I32), w_words.rearrange("a p b -> p a b").bitcast(I32))
-        for q in range(4):
+        for group in range(4):
             nc.sync.dma_start(
-                planes[QUAD * q : QUAD * q + 4, :, :].bitcast(I32),
-                picked_scales[ROWS + 8 * q : ROWS + 8 * q + 8, :].bitcast(I32),
+                planes[QUAD * group : QUAD * group + 4, :, :].bitcast(I32),
+                picked_scales[SCALE_ROWS + 8 * group : SCALE_ROWS + 8 * group + 8, :].bitcast(I32),
             )
 
         wx_rows = wx.rearrange("(p t) n -> p t n", t=PACK)
         x_rows = x.rearrange("(p t) j -> p t j", t=PACK)
-        raw = late.tile([P, 4 * PACK * HALF], F32, name="raw", offset=4 * N, align_bytes=64)
         wx_raw = [
-            raw[:, PACK * HALF * h : PACK * HALF * (h + 1)].rearrange("p (t c) -> p t c", t=PACK) for h in range(2)
+            placed.tile([P, PACK, HALF], F32, name="wx_raw%d" % h, offset=h * 2 * (RAW - ALIGN), align_bytes=ALIGN)
+            for h in range(2)
         ]
         for h in range(2):
-            nc.sync.dma_start(wx_raw[h], wx_rows[:, :, HALF * h : HALF * (h + 1)])
-        x_all = raw[:, PACK * N : PACK * (N + J)].rearrange("p (t c) -> p t c", t=PACK)
-        nc.sync.dma_start(x_all, x_rows)
+            nc.sync.dma_start(wx_raw[h][:], wx_rows[:, :, HALF * h : HALF * (h + 1)])
+        x_all = sbuf([P, PACK, J], F32, "x_all", slot="picked_scales")
+        nc.sync.dma_start(x_all[:], x_rows)
         x_raw = [x_all[:, :, HALF * h : HALF * (h + 1)] for h in range(2)]
 
         picked = sbuf([P, J + HALF], U32, "picked")
@@ -116,35 +120,36 @@ def tile_list_interp_none_kernel(
                 picked[:, lo : lo + J], table[:].bitcast(U32).indirect(offsets[:, LIST_COLS * g : LIST_COLS * (g + 1)])
             )
 
-        def part(g, h):
-            lo = HALF * (1 - g + h)
-            parted = sbuf([P, 2 * 2 * HALF], U8, "parted%d%d" % (g, h))
+        def part(g, lo, hi):
+            width = P * (hi - lo)
+            start = HALF * (1 - g) + P * lo
+            parted = sbuf([P, 2 * 2 * width], U8, "parted%d%d" % (g, lo))
             nc.vector.tensor_copy(
                 parted[:].bitcast(U16).rearrange("p (a j) -> p a j", a=2),
-                picked[:, lo : lo + HALF].bitcast(U16).rearrange("p (j a) -> p a j", a=2),
+                picked[:, start : start + width].bitcast(U16).rearrange("p (j a) -> p a j", a=2),
             )
-            for i in range(2):
+            for jt in range(lo, hi):
                 for a in range(2):
-                    first_byte = 2 * (a * HALF + P * i)
-                    tab_codes[g, a, 2 * h + i] = parted[:, first_byte : first_byte + 2 * P]
+                    first_byte = 2 * (a * width + P * (jt - lo))
+                    tab_codes[g, a, jt] = parted[:, first_byte : first_byte + 2 * P]
 
         gather(0)
-        part(0, 0)
-        part(0, 1)
+        part(0, 0, 2)
+        part(0, 2, 3)
         gather(1)
-        part(1, 0)
-        part(1, 1)
+        part(0, 3, 4)
+        part(1, 0, 4)
 
         def project(g, jt, acc):
-            for a in (1, 0):
+            for a in range(2):
                 nc.tensor.matmul_mx(
                     out=acc[:],
                     lhsT=tab_codes[g, a, jt].bitcast(FP4X4),
                     lhsT_scale=planes[:, a, g * J + P * jt : g * J + P * (jt + 1)],
                     rhs=w_codes[:, a, :].bitcast(FP4X4),
                     rhs_scale=w_planes[:, a * N : (a + 1) * N],
-                    start=(a == 1),
-                    stop=(a == 0),
+                    start=(a == 0),
+                    stop=(a == 1),
                 )
 
         def interleave(copy, rows, grouped):
@@ -166,7 +171,7 @@ def tile_list_interp_none_kernel(
         x_codes = sbuf([P, J], U32, "x_codes")
         x_scales = sbuf([P, J], U8, "x_scales")
 
-        warm_up = bank([P, N], 6, "warm_up")
+        warm_up = bank([P, N], 2 * TILES - 2, "warm_up")
         table_bytes = table[:, T // 2 : T].bitcast(U8)
         for a in range(2):
             nc.tensor.matmul_mx(
@@ -179,7 +184,7 @@ def tile_list_interp_none_kernel(
                 stop=(a == 1),
             )
 
-        iw_bank = bank([P, P], 7, "iw_bank")
+        iw_bank = bank([P, P], 2 * TILES - 1, "iw_bank")
         nc.tensor.transpose(iw_bank[:], iw_rows[:], ident[:])
         iw_cols = [sbuf([P, TILES], F32, "iw_cols%d" % g) for g in range(2)]
         for g in range(2):
@@ -195,9 +200,9 @@ def tile_list_interp_none_kernel(
             first[jt] = sbuf([P, N], F32, "first%d" % jt)
             nc.scalar.activation(first[jt][:], a0[jt][:], COPY, scale=iw_cols[0][:, jt : jt + 1])
 
-        def weigh_second(jt, lo=0, hi=N):
+        def weigh_second(jt):
             nc.vector.scalar_tensor_tensor(
-                both[jt][:, lo:hi], a1[jt][:, lo:hi], iw_cols[1][:, jt : jt + 1], first[jt][:, lo:hi], MULT, ADD
+                both[jt][:], a1[jt][:], iw_cols[1][:, jt : jt + 1], first[jt][:], MULT, ADD
             )
 
         def finish(h):
@@ -236,10 +241,10 @@ def tile_list_interp_none_kernel(
             project(1, jt, a1[jt])
 
         wx_grouped = [sbuf([P, HALF, PACK], BF16, "wx_grouped%d" % h) for h in range(2)]
-        wx_lo = interleave(nc.scalar.copy, wx_raw[0], wx_grouped[0][:])
+        wx_lo = interleave(nc.scalar.copy, wx_raw[0][:], wx_grouped[0][:])
         for jt in range(TILES):
             weigh_first(jt)
-        wx_hi = interleave(nc.vector.tensor_copy, wx_raw[1], wx_grouped[1][:])
+        wx_hi = interleave(nc.vector.tensor_copy, wx_raw[1][:], wx_grouped[1][:])
         quantize(wx_lo, wx_codes, wx_scales, 0)
         quantize(wx_hi, wx_codes, wx_scales, 1)
 

@@ -65,6 +65,8 @@ def tile_list_interp_none_kernel(
             )
 
         nc.scalar.dma_start(table[:, T // 2 : T], table_words[:, T // 2 : T])
+        w_codes = sbuf([P, 2, 2 * N], U8, "w_codes")
+        nc.scalar.dma_start(w_codes[:].bitcast(I32), w_words.rearrange("a p b -> p a b").bitcast(I32))
 
         nc.vector.memset(scale_table[0:SCALE_ROWS, :].bitcast(I32), 0)
         planes = sbuf([P, 2, 2 * J], U8, "planes")
@@ -91,8 +93,6 @@ def tile_list_interp_none_kernel(
         picked_scales = sbuf([P, 2 * J], U8, "picked_scales")
         nc.vector.tensor_copy(picked_scales[:], scale_table[:].indirect(offsets[:]))
 
-        w_codes = placed.tile([P, 2, 2 * N], U8, name="w_codes", offset=RAW, align_bytes=ALIGN)
-        nc.sync.dma_start(w_codes[:].bitcast(I32), w_words.rearrange("a p b -> p a b").bitcast(I32))
         for group in range(4):
             nc.sync.dma_start(
                 planes[QUAD * group : QUAD * group + 4, :, :].bitcast(I32),
@@ -227,7 +227,7 @@ def tile_list_interp_none_kernel(
                         start=True,
                         stop=True,
                     )
-                cuts = (0, 1, 2) if (h, m) == (1, 1) else (0, 2)
+                cuts = (0, 1, 2)
                 for lo, hi in zip(cuts, cuts[1:]):
                     looked_up = sbuf([P, hi - lo, HALF], F32, "looked_up%d%d%d" % (h, m, lo))
                     nc.scalar.copy(looked_up[:], turned[m][:, lo:hi, :])

@@ -22,7 +22,7 @@ PACK = 4
 QUAD = 32
 TILES = 4
 HALF = 256
-SCALE_ROWS = 96
+SCALE_ROWS = (48, 112)
 RAW = 4 * PACK * HALF
 ALIGN = 64
 LIST_COLS = J // 16
@@ -47,9 +47,11 @@ def tile_list_interp_none_kernel(
         nc.sync.dma_start(offsets[:], offs)
 
         scale_table = placed.tile([P, T], U8, name="scale_table", offset=RAW - ALIGN, align_bytes=ALIGN)
-        nc.scalar.dma_start(
-            scale_table[SCALE_ROWS:P, :].bitcast(I32), tab_scales.bitcast(I32).rearrange("a q t -> q a t")
-        )
+        scale_rows = tab_scales.bitcast(I32).rearrange("a q t -> q a t")
+        for half, queue in enumerate((nc.scalar, nc.sync)):
+            queue.dma_start(
+                scale_table[SCALE_ROWS[half] : SCALE_ROWS[half] + 16, :].bitcast(I32), scale_rows[8 * half : 8 * half + 8]
+            )
 
         table = sbuf([P, T], I32, "table")
         table_words = tab_words[0].rearrange("p t b -> p (t b)").bitcast(I32)
@@ -58,7 +60,7 @@ def tile_list_interp_none_kernel(
         w_planes = sbuf([P, 2 * N], U8, "w_planes")
         nc.vector.memset(w_planes[:, 0:N].bitcast(I32), 0)
         nc.gpsimd.memset(w_planes[:, N : 2 * N].bitcast(I32), 0)
-        for r, queue in enumerate((nc.sync, nc.scalar, nc.sync, nc.scalar)):
+        for r, queue in enumerate((nc.gpsimd, nc.sync, nc.scalar, nc.scalar)):
             queue.dma_start(
                 w_planes[r:P:QUAD, :].bitcast(I32).rearrange("q (a n) -> q a n", a=2),
                 w_scales.bitcast(I32)[:, r:16:4, :].rearrange("a q n -> q a n"),
@@ -68,7 +70,8 @@ def tile_list_interp_none_kernel(
         w_codes = sbuf([P, 2, 2 * N], U8, "w_codes")
         nc.scalar.dma_start(w_codes[:].bitcast(I32), w_words.rearrange("a p b -> p a b").bitcast(I32))
 
-        nc.vector.memset(scale_table[0:SCALE_ROWS, :].bitcast(I32), 0)
+        for first_row in SCALE_ROWS:
+            nc.vector.memset(scale_table[first_row - 48 : first_row, :].bitcast(I32), 0)
         planes = sbuf([P, 2, 2 * J], U8, "planes")
         nc.vector.memset(planes[:].bitcast(I32), 0)
 
@@ -94,9 +97,10 @@ def tile_list_interp_none_kernel(
         nc.vector.tensor_copy(picked_scales[:], scale_table[:].indirect(offsets[:]))
 
         for group in range(4):
+            source = SCALE_ROWS[group // 2] + 8 * (group % 2)
             nc.sync.dma_start(
                 planes[QUAD * group : QUAD * group + 4, :, :].bitcast(I32),
-                picked_scales[SCALE_ROWS + 8 * group : SCALE_ROWS + 8 * group + 8, :].bitcast(I32),
+                picked_scales[source : source + 8, :].bitcast(I32),
             )
 
         wx_rows = wx.rearrange("(p t) n -> p t n", t=PACK)
@@ -113,16 +117,18 @@ def tile_list_interp_none_kernel(
 
         picked = sbuf([P, J + HALF], U32, "picked")
         tab_codes = {}
+        place = {(0, 0): P, (0, 1): 2 * P, (0, 2): 0, (0, 3): P}
+        place.update({(1, jt): HALF + P * jt for jt in range(TILES)})
 
-        def gather(g):
-            lo = HALF * (1 - g)
+        def gather(g, lo, hi):
+            cols = slice(LIST_COLS * g + 8 * lo, LIST_COLS * g + 8 * hi)
             nc.vector.tensor_copy(
-                picked[:, lo : lo + J], table[:].bitcast(U32).indirect(offsets[:, LIST_COLS * g : LIST_COLS * (g + 1)])
+                picked[:, place[g, lo] : place[g, lo] + P * (hi - lo)], table[:].bitcast(U32).indirect(offsets[:, cols])
             )
 
         def part(g, lo, hi):
             width = P * (hi - lo)
-            start = HALF * (1 - g) + P * lo
+            start = place[g, lo]
             parted = sbuf([P, 2 * 2 * width], U8, "parted%d%d" % (g, lo))
             nc.vector.tensor_copy(
                 parted[:].bitcast(U16).rearrange("p (a j) -> p a j", a=2),
@@ -133,11 +139,12 @@ def tile_list_interp_none_kernel(
                     first_byte = 2 * (a * width + P * (jt - lo))
                     tab_codes[g, a, jt] = parted[:, first_byte : first_byte + 2 * P]
 
-        gather(0)
-        part(0, 0, 2)
-        part(0, 2, 3)
-        gather(1)
-        part(0, 3, 4)
+        gather(0, 0, 2)
+        part(0, 0, 1)
+        part(0, 1, 2)
+        gather(0, 2, 4)
+        gather(1, 0, 4)
+        part(0, 2, 4)
         part(1, 0, 4)
 
         def project(g, jt, acc):

@@ -24,7 +24,9 @@ TILES = 4
 HALF = 256
 SCALE_ROWS = (48, 112)
 RAW = 4 * PACK * HALF
+BANK = 2048
 ALIGN = 64
+SPLIT = 3 * T // 8
 LIST_COLS = J // 16
 
 
@@ -41,7 +43,7 @@ def tile_list_interp_none_kernel(
             return keep.tile(shape, dtype, name=name, tag=slot or name, align_bytes=ALIGN)
 
         def bank(shape, index, name):
-            return psum.tile(shape, F32, name=name, tag="bank%d" % index)
+            return psum.tile(shape, F32, name=name, offset=BANK * index)
 
         offsets = keep.tile([P, 2 * LIST_COLS], U16, name="offsets")
         nc.sync.dma_start(offsets[:], offs)
@@ -55,31 +57,10 @@ def tile_list_interp_none_kernel(
 
         table = sbuf([P, T], I32, "table")
         table_words = tab_words[0].rearrange("p t b -> p (t b)").bitcast(I32)
-        nc.scalar.dma_start(table[:, 0 : T // 2], table_words[:, 0 : T // 2])
-
-        w_planes = sbuf([P, 2 * N], U8, "w_planes")
-        nc.vector.memset(w_planes[:, 0:N].bitcast(I32), 0)
-        nc.gpsimd.memset(w_planes[:, N : 2 * N].bitcast(I32), 0)
-        for r, queue in enumerate((nc.gpsimd, nc.sync, nc.scalar, nc.scalar)):
-            queue.dma_start(
-                w_planes[r:P:QUAD, :].bitcast(I32).rearrange("q (a n) -> q a n", a=2),
-                w_scales.bitcast(I32)[:, r:16:4, :].rearrange("a q n -> q a n"),
-            )
-
-        nc.scalar.dma_start(table[:, T // 2 : T], table_words[:, T // 2 : T])
-        w_codes = sbuf([P, 2, 2 * N], U8, "w_codes")
-        nc.scalar.dma_start(w_codes[:].bitcast(I32), w_words.rearrange("a p b -> p a b").bitcast(I32))
-
-        for first_row in SCALE_ROWS:
-            nc.vector.memset(scale_table[first_row - 48 : first_row, :].bitcast(I32), 0)
-        planes = sbuf([P, 2, 2 * J], U8, "planes")
-        nc.vector.memset(planes[:].bitcast(I32), 0)
+        nc.scalar.dma_start(table[:, 0:SPLIT], table_words[:, 0:SPLIT])
 
         iw_rows = sbuf([P, P], F32, "iw_rows")
         nc.gpsimd.memset(iw_rows[:], 0.0)
-        nc.gpsimd.dma_start(iw_rows[0:TILES, :], iw0.rearrange("(c p) -> c p", p=P))
-        nc.gpsimd.dma_start(iw_rows[TILES : 2 * TILES, :], iw1.rearrange("(c p) -> c p", p=P))
-
         zeros = sbuf([P, P], F32, "zeros")
         nc.gpsimd.memset(zeros[:], 0.0)
         ident = sbuf([P, P], F32, "ident")
@@ -93,9 +74,29 @@ def tile_list_interp_none_kernel(
             channel_multiplier=1,
         )
 
+        w_planes = sbuf([P, 2 * N], U8, "w_planes")
+        nc.vector.memset(w_planes[:, 0:N].bitcast(I32), 0)
+        nc.gpsimd.memset(w_planes[:, N : 2 * N].bitcast(I32), 0)
+        for r, queue in enumerate((nc.gpsimd, nc.gpsimd, nc.gpsimd, nc.sync)):
+            queue.dma_start(
+                w_planes[r:P:QUAD, :].bitcast(I32).rearrange("q (a n) -> q a n", a=2),
+                w_scales.bitcast(I32)[:, r:16:4, :].rearrange("a q n -> q a n"),
+            )
+
+        nc.scalar.dma_start(iw_rows[0:TILES, :], iw0.rearrange("(c p) -> c p", p=P))
+        nc.scalar.dma_start(iw_rows[TILES : 2 * TILES, :], iw1.rearrange("(c p) -> c p", p=P))
+        nc.scalar.dma_start(table[:, SPLIT:T], table_words[:, SPLIT:T])
+        w_codes = sbuf([P, 2, 2 * N], U8, "w_codes")
+        nc.scalar.dma_start(w_codes[:].bitcast(I32), w_words.rearrange("a p b -> p a b").bitcast(I32))
+
+        for first_row in SCALE_ROWS:
+            nc.vector.memset(scale_table[first_row - 48 : first_row, :].bitcast(I32), 0)
+
+
         picked_scales = sbuf([P, 2 * J], U8, "picked_scales")
         nc.vector.tensor_copy(picked_scales[:], scale_table[:].indirect(offsets[:]))
 
+        planes = placed.tile([P, 2, 2 * J], U8, name="planes", offset=RAW, align_bytes=ALIGN)
         for group in range(4):
             source = SCALE_ROWS[group // 2] + 8 * (group % 2)
             nc.sync.dma_start(
@@ -105,14 +106,13 @@ def tile_list_interp_none_kernel(
 
         wx_rows = wx.rearrange("(p t) n -> p t n", t=PACK)
         x_rows = x.rearrange("(p t) j -> p t j", t=PACK)
-        wx_raw = [
-            placed.tile([P, PACK, HALF], F32, name="wx_raw%d" % h, offset=h * 2 * (RAW - ALIGN), align_bytes=ALIGN)
-            for h in range(2)
-        ]
+        early = placed.tile([P, PACK * HALF], F32, name="early", offset=0, align_bytes=ALIGN)
+        late = placed.tile([P, PACK * (HALF + J)], F32, name="late", offset=2 * (RAW - ALIGN), align_bytes=ALIGN)
+        wx_raw = [tile[:, 0 : PACK * HALF].rearrange("p (t c) -> p t c", t=PACK) for tile in (early, late)]
         for h in range(2):
-            nc.sync.dma_start(wx_raw[h][:], wx_rows[:, :, HALF * h : HALF * (h + 1)])
-        x_all = sbuf([P, PACK, J], F32, "x_all", slot="picked_scales")
-        nc.sync.dma_start(x_all[:], x_rows)
+            nc.sync.dma_start(wx_raw[h], wx_rows[:, :, HALF * h : HALF * (h + 1)])
+        x_all = late[:, PACK * HALF :].rearrange("p (t c) -> p t c", t=PACK)
+        nc.sync.dma_start(x_all, x_rows)
         x_raw = [x_all[:, :, HALF * h : HALF * (h + 1)] for h in range(2)]
 
         picked = sbuf([P, J + HALF], U32, "picked")
@@ -178,24 +178,24 @@ def tile_list_interp_none_kernel(
         x_codes = sbuf([P, J], U32, "x_codes")
         x_scales = sbuf([P, J], U8, "x_scales")
 
-        warm_up = bank([P, N], 2 * TILES - 2, "warm_up")
-        table_bytes = table[:, T // 2 : T].bitcast(U8)
-        for a in range(2):
-            nc.tensor.matmul_mx(
-                out=warm_up[:],
-                lhsT=table_bytes[:, 0 : 2 * P].bitcast(FP4X4),
-                lhsT_scale=w_planes[:, 0:P],
-                rhs=table_bytes[:, 0 : 2 * N].bitcast(FP4X4),
-                rhs_scale=w_planes[:, 0:N],
-                start=(a == 0),
-                stop=(a == 1),
-            )
-
-        iw_bank = bank([P, P], 2 * TILES - 1, "iw_bank")
-        nc.tensor.transpose(iw_bank[:], iw_rows[:], ident[:])
+        iw_bank = bank([P, 2 * TILES * N], 0, "iw_bank")
+        nc.tensor.transpose(iw_bank[:, 0:P], iw_rows[:], ident[:])
         iw_cols = [sbuf([P, TILES], F32, "iw_cols%d" % g) for g in range(2)]
         for g in range(2):
             nc.scalar.activation(iw_cols[g][:], iw_bank[:, TILES * g : TILES * (g + 1)], COPY)
+
+        table_bytes = table[:, 0:SPLIT].bitcast(U8)
+        for index in range(2):
+            warm_up = bank([P, N], index, "warm_up%d" % index)
+            nc.tensor.matmul_mx(
+                out=warm_up[:],
+                lhsT=table_bytes[:, 0 : 2 * P].bitcast(FP4X4),
+                lhsT_scale=picked_scales[:, 0:P],
+                rhs=table_bytes[:, 0 : 2 * N].bitcast(FP4X4),
+                rhs_scale=picked_scales[:, 0:N],
+                start=True,
+                stop=True,
+            )
 
         a0 = [bank([P, N], jt, "a0_%d" % jt) for jt in range(TILES)]
         a1 = [bank([P, N], TILES + jt, "a1_%d" % jt) for jt in range(TILES)]
@@ -248,10 +248,10 @@ def tile_list_interp_none_kernel(
             project(1, jt, a1[jt])
 
         wx_grouped = [sbuf([P, HALF, PACK], BF16, "wx_grouped%d" % h) for h in range(2)]
-        wx_lo = interleave(nc.scalar.copy, wx_raw[0][:], wx_grouped[0][:])
+        wx_lo = interleave(nc.scalar.copy, wx_raw[0], wx_grouped[0][:])
         for jt in range(TILES):
             weigh_first(jt)
-        wx_hi = interleave(nc.vector.tensor_copy, wx_raw[1][:], wx_grouped[1][:])
+        wx_hi = interleave(nc.vector.tensor_copy, wx_raw[1], wx_grouped[1][:])
         quantize(wx_lo, wx_codes, wx_scales, 0)
         quantize(wx_hi, wx_codes, wx_scales, 1)
 

@@ -48,7 +48,7 @@ def tile_list_interp_none_kernel(
         offsets = keep.tile([P, 2 * LIST_COLS], U16, name="offsets")
         nc.sync.dma_start(offsets[:], offs)
 
-        scale_table = placed.tile([P, T], U8, name="scale_table", offset=RAW - ALIGN, align_bytes=ALIGN)
+        scale_table = placed.tile([P, T], U8, name="scale_table", offset=0, align_bytes=ALIGN)
         scale_rows = tab_scales.bitcast(I32).rearrange("a q t -> q a t")
         for half, queue in enumerate((nc.scalar, nc.sync)):
             queue.dma_start(
@@ -59,7 +59,7 @@ def tile_list_interp_none_kernel(
         table_words = tab_words[0].rearrange("p t b -> p (t b)").bitcast(I32)
         nc.scalar.dma_start(table[:, 0:SPLIT], table_words[:, 0:SPLIT])
 
-        iw_rows = sbuf([P, P], F32, "iw_rows")
+        iw_rows = placed.tile([P, P], F32, name="iw_rows", offset=T, align_bytes=ALIGN)
         nc.gpsimd.memset(iw_rows[:], 0.0)
         zeros = sbuf([P, P], F32, "zeros")
         nc.gpsimd.memset(zeros[:], 0.0)
@@ -89,6 +89,11 @@ def tile_list_interp_none_kernel(
         w_codes = sbuf([P, 2, 2 * N], U8, "w_codes")
         nc.scalar.dma_start(w_codes[:].bitcast(I32), w_words.rearrange("a p b -> p a b").bitcast(I32))
 
+        iw_bank = bank([P, 2 * TILES * N], 0, "iw_bank")
+        nc.tensor.transpose(iw_bank[:, 0:P], iw_rows[:], ident[:])
+        iw_cols = [sbuf([P, TILES], F32, "iw_cols%d" % g) for g in range(2)]
+        nc.scalar.activation(iw_cols[0][:], iw_bank[:, 0:TILES], COPY)
+
         for first_row in SCALE_ROWS:
             nc.vector.memset(scale_table[first_row - 48 : first_row, :].bitcast(I32), 0)
 
@@ -96,23 +101,24 @@ def tile_list_interp_none_kernel(
         picked_scales = sbuf([P, 2 * J], U8, "picked_scales")
         nc.vector.tensor_copy(picked_scales[:], scale_table[:].indirect(offsets[:]))
 
-        planes = placed.tile([P, 2, 2 * J], U8, name="planes", offset=RAW, align_bytes=ALIGN)
-        for group in range(4):
+        planes = placed.tile([P, 2, 2 * J], U8, name="planes", offset=T + ALIGN - 4 * J, align_bytes=ALIGN)
+        for group in (0, 2, 1, 3):
             source = SCALE_ROWS[group // 2] + 8 * (group % 2)
-            nc.sync.dma_start(
+            nc.scalar.dma_start(
                 planes[QUAD * group : QUAD * group + 4, :, :].bitcast(I32),
                 picked_scales[source : source + 8, :].bitcast(I32),
             )
 
+        nc.scalar.activation(iw_cols[1][:], iw_bank[:, TILES : 2 * TILES], COPY)
+
         wx_rows = wx.rearrange("(p t) n -> p t n", t=PACK)
         x_rows = x.rearrange("(p t) j -> p t j", t=PACK)
-        early = placed.tile([P, PACK * HALF], F32, name="early", offset=0, align_bytes=ALIGN)
-        late = placed.tile([P, PACK * (HALF + J)], F32, name="late", offset=2 * (RAW - ALIGN), align_bytes=ALIGN)
-        wx_raw = [tile[:, 0 : PACK * HALF].rearrange("p (t c) -> p t c", t=PACK) for tile in (early, late)]
+        late = placed.tile([P, PACK * (N + J)], F32, name="late", offset=T + 4 * P - ALIGN, align_bytes=ALIGN)
+        wx_raw = [late[:, PACK * HALF * h : PACK * HALF * (h + 1)].rearrange("p (t c) -> p t c", t=PACK) for h in range(2)]
         for h in range(2):
-            nc.sync.dma_start(wx_raw[h], wx_rows[:, :, HALF * h : HALF * (h + 1)])
-        x_all = late[:, PACK * HALF :].rearrange("p (t c) -> p t c", t=PACK)
-        nc.sync.dma_start(x_all, x_rows)
+            nc.scalar.dma_start(wx_raw[h], wx_rows[:, :, HALF * h : HALF * (h + 1)])
+        x_all = late[:, PACK * N :].rearrange("p (t c) -> p t c", t=PACK)
+        nc.scalar.dma_start(x_all, x_rows)
         x_raw = [x_all[:, :, HALF * h : HALF * (h + 1)] for h in range(2)]
 
         picked = sbuf([P, J + HALF], U32, "picked")
@@ -177,12 +183,6 @@ def tile_list_interp_none_kernel(
         wx_scales = sbuf([P, N], U8, "wx_scales")
         x_codes = sbuf([P, J], U32, "x_codes")
         x_scales = sbuf([P, J], U8, "x_scales")
-
-        iw_bank = bank([P, 2 * TILES * N], 0, "iw_bank")
-        nc.tensor.transpose(iw_bank[:, 0:P], iw_rows[:], ident[:])
-        iw_cols = [sbuf([P, TILES], F32, "iw_cols%d" % g) for g in range(2)]
-        for g in range(2):
-            nc.scalar.activation(iw_cols[g][:], iw_bank[:, TILES * g : TILES * (g + 1)], COPY)
 
         table_bytes = table[:, 0:SPLIT].bitcast(U8)
         for index in range(2):

@@ -27,6 +27,7 @@ RAW = 4 * PACK * HALF
 BANK = 2048
 ALIGN = 64
 SPLIT = 3 * T // 8
+SHARE = 160
 LIST_COLS = J // 16
 
 
@@ -114,12 +115,14 @@ def tile_list_interp_none_kernel(
         wx_rows = wx.rearrange("(p t) n -> p t n", t=PACK)
         x_rows = x.rearrange("(p t) j -> p t j", t=PACK)
         late = placed.tile([P, PACK * (N + J)], F32, name="late", offset=T + 4 * P - ALIGN, align_bytes=ALIGN)
-        wx_raw = [late[:, PACK * HALF * h : PACK * HALF * (h + 1)].rearrange("p (t c) -> p t c", t=PACK) for h in range(2)]
+        wx_raw = late[:, 0 : PACK * N].rearrange("p (t c) -> p t c", t=PACK)
+        nc.scalar.dma_start(wx_raw, wx_rows)
+        x_raw = [
+            late[:, PACK * (N + HALF * h) : PACK * (N + HALF * (h + 1))].rearrange("p (t c) -> p t c", t=PACK)
+            for h in range(2)
+        ]
         for h in range(2):
-            nc.scalar.dma_start(wx_raw[h], wx_rows[:, :, HALF * h : HALF * (h + 1)])
-        x_all = late[:, PACK * N :].rearrange("p (t c) -> p t c", t=PACK)
-        nc.scalar.dma_start(x_all, x_rows)
-        x_raw = [x_all[:, :, HALF * h : HALF * (h + 1)] for h in range(2)]
+            nc.scalar.dma_start(x_raw[h], x_rows[:, :, HALF * h : HALF * (h + 1)])
 
         picked = sbuf([P, J + HALF], U32, "picked")
         tab_codes = {}
@@ -200,7 +203,10 @@ def tile_list_interp_none_kernel(
         a0 = [bank([P, N], jt, "a0_%d" % jt) for jt in range(TILES)]
         a1 = [bank([P, N], TILES + jt, "a1_%d" % jt) for jt in range(TILES)]
         first = {}
-        both = [sbuf([P, N], F32, "both%d" % jt) for jt in range(TILES - 1)]
+        both = [wx_raw[:, 0:2, 0:HALF]]
+        for jt in range(1, TILES - 1):
+            both.append(sbuf([P, 2, HALF], F32, "both%d" % jt)[:])
+        both.append(x_raw[0][:, 0:2, :])
         out_by_tile = out.rearrange("(nt p) j -> p nt j", p=P)
 
         def weigh_first(jt):
@@ -209,7 +215,12 @@ def tile_list_interp_none_kernel(
 
         def weigh_second(jt):
             nc.vector.scalar_tensor_tensor(
-                both[jt][:], a1[jt][:], iw_cols[1][:, jt : jt + 1], first[jt][:], MULT, ADD
+                both[jt],
+                a1[jt][:].rearrange("p (m c) -> p m c", m=2),
+                iw_cols[1][:, jt : jt + 1],
+                first[jt][:].rearrange("p (m c) -> p m c", m=2),
+                MULT,
+                ADD,
             )
 
         def finish(h):
@@ -218,7 +229,7 @@ def tile_list_interp_none_kernel(
                 for nt in range(TILES):
                     nc.tensor.transpose(
                         turned[nt // 2][:, nt % 2, P * (jt % 2) : P * (jt % 2 + 1)],
-                        both[jt][:, P * nt : P * (nt + 1)],
+                        both[jt][:, nt // 2, P * (nt % 2) : P * (nt % 2 + 1)],
                         ident[:],
                     )
             for m in range(2):
@@ -247,21 +258,25 @@ def tile_list_interp_none_kernel(
         for jt in range(TILES):
             project(1, jt, a1[jt])
 
-        wx_grouped = [sbuf([P, HALF, PACK], BF16, "wx_grouped%d" % h) for h in range(2)]
-        wx_lo = interleave(nc.scalar.copy, wx_raw[0], wx_grouped[0][:])
+        wx_grouped = sbuf([P, N * PACK], BF16, "wx_grouped")
+        wx_by_column = wx_grouped[:].rearrange("p (c t) -> p c t", t=PACK)
         for jt in range(TILES):
             weigh_first(jt)
-        wx_hi = interleave(nc.vector.tensor_copy, wx_raw[1], wx_grouped[1][:])
-        quantize(wx_lo, wx_codes, wx_scales, 0)
-        quantize(wx_hi, wx_codes, wx_scales, 1)
+        interleave(nc.scalar.copy, wx_raw[:, :, N - SHARE : N], wx_by_column[:, N - SHARE : N, :])
+        for lo, hi in ((0, HALF), (HALF, N - SHARE)):
+            interleave(nc.vector.tensor_copy, wx_raw[:, :, lo:hi], wx_by_column[:, lo:hi, :])
+        quantize(wx_by_column[:, 0:HALF, :], wx_codes, wx_scales, 0)
 
         x_grouped = sbuf([P, 2 * HALF * PACK], BF16, "x_grouped", slot="iw_cols0")
-        both.append(x_grouped[:, 0 : HALF * PACK].bitcast(F32))
+        x_by_column = x_grouped[:].rearrange("p (c t) -> p c t", t=PACK)
         for h in range(2):
-            grouped = x_grouped[:, HALF * PACK * h : HALF * PACK * (h + 1)].rearrange("p (c t) -> p c t", t=PACK)
-            interleave(nc.scalar.copy, x_raw[h], grouped)
-            weigh_second(2 * h)
-            weigh_second(2 * h + 1)
-            quantize(grouped, x_codes, x_scales, h)
+            interleave(nc.scalar.copy, x_raw[h], x_by_column[:, HALF * h : HALF * (h + 1), :])
+        weigh_second(0)
+        quantize(wx_by_column[:, HALF:N, :], wx_codes, wx_scales, 1)
+        weigh_second(1)
+        weigh_second(2)
+        quantize(x_by_column[:, 0:HALF, :], x_codes, x_scales, 0)
+        weigh_second(3)
+        quantize(x_by_column[:, HALF:J, :], x_codes, x_scales, 1)
         for h in range(2):
             finish(h)

@@ -26,7 +26,7 @@ SCALE_ROWS = (48, 112)
 RAW = 4 * PACK * HALF
 BANK = 2048
 ALIGN = 64
-SPLIT = 3 * T // 8
+SPLIT = 25 * T // 32
 SHARE = 160
 LIST_COLS = J // 16
 
@@ -58,10 +58,12 @@ def tile_list_interp_none_kernel(
 
         table = sbuf([P, T], I32, "table")
         table_words = tab_words[0].rearrange("p t b -> p (t b)").bitcast(I32)
-        nc.scalar.dma_start(table[:, 0:SPLIT], table_words[:, 0:SPLIT])
 
         iw_rows = placed.tile([P, P], F32, name="iw_rows", offset=T, align_bytes=ALIGN)
         nc.gpsimd.memset(iw_rows[:], 0.0)
+        nc.scalar.dma_start(iw_rows[0:TILES, :], iw0.rearrange("(c p) -> c p", p=P))
+        nc.scalar.dma_start(iw_rows[TILES : 2 * TILES, :], iw1.rearrange("(c p) -> c p", p=P))
+        nc.scalar.dma_start(table[:, 0:SPLIT], table_words[:, 0:SPLIT])
         zeros = sbuf([P, P], F32, "zeros")
         nc.gpsimd.memset(zeros[:], 0.0)
         ident = sbuf([P, P], F32, "ident")
@@ -84,8 +86,6 @@ def tile_list_interp_none_kernel(
                 w_scales.bitcast(I32)[:, r:16:4, :].rearrange("a q n -> q a n"),
             )
 
-        nc.scalar.dma_start(iw_rows[0:TILES, :], iw0.rearrange("(c p) -> c p", p=P))
-        nc.scalar.dma_start(iw_rows[TILES : 2 * TILES, :], iw1.rearrange("(c p) -> c p", p=P))
         nc.scalar.dma_start(table[:, SPLIT:T], table_words[:, SPLIT:T])
         w_codes = sbuf([P, 2, 2 * N], U8, "w_codes")
         nc.scalar.dma_start(w_codes[:].bitcast(I32), w_words.rearrange("a p b -> p a b").bitcast(I32))

@@ -27,6 +27,7 @@ RAW = 4 * PACK * HALF
 BANK = 2048
 ALIGN = 64
 SPLIT = 25 * T // 32
+LINE = 256
 SHARE = 160
 LIST_COLS = J // 16
 
@@ -41,7 +42,7 @@ def tile_list_interp_none_kernel(
         psum = ctx.enter_context(tc.psum_pool(name="psum", bufs=1))
 
         def sbuf(shape, dtype, name, slot=None):
-            return keep.tile(shape, dtype, name=name, tag=slot or name, align_bytes=ALIGN)
+            return keep.tile(shape, dtype, name=name, tag=slot or name, align_bytes=LINE)
 
         def bank(shape, index, name):
             return psum.tile(shape, F32, name=name, offset=BANK * index)
@@ -102,7 +103,7 @@ def tile_list_interp_none_kernel(
         picked_scales = sbuf([P, 2 * J], U8, "picked_scales")
         nc.vector.tensor_copy(picked_scales[:], scale_table[:].indirect(offsets[:]))
 
-        planes = placed.tile([P, 2, 2 * J], U8, name="planes", offset=T + ALIGN - 4 * J, align_bytes=ALIGN)
+        planes = placed.tile([P, 2, 2 * J], U8, name="planes", offset=T + LINE - 4 * J, align_bytes=LINE)
         for group in (0, 2, 1, 3):
             source = SCALE_ROWS[group // 2] + 8 * (group % 2)
             nc.scalar.dma_start(

@@ -23,13 +23,13 @@ QUAD = 32
 TILES = 4
 HALF = 256
 SCALE_ROWS = (48, 112)
-RAW = 4 * PACK * HALF
+IW_ROW = P - 2 * TILES
 BANK = 2048
 ALIGN = 64
-SPLIT = 25 * T // 32
 LINE = 256
-SHARE = 160
 LIST_COLS = J // 16
+TABLE_CUTS = (0, T // 2, 7 * T // 8, T)
+SHARE = 64
 
 
 def tile_list_interp_none_kernel(
@@ -50,95 +50,99 @@ def tile_list_interp_none_kernel(
         offsets = keep.tile([P, 2 * LIST_COLS], U16, name="offsets")
         nc.sync.dma_start(offsets[:], offs)
 
-        scale_table = placed.tile([P, T], U8, name="scale_table", offset=0, align_bytes=ALIGN)
+        scale_table = placed.tile([P, T], U8, name="scale_table", offset=0, align_bytes=LINE)
         scale_rows = tab_scales.bitcast(I32).rearrange("a q t -> q a t")
-        for half, queue in enumerate((nc.scalar, nc.sync)):
+        for half, queue in enumerate((nc.scalar, nc.scalar)):
             queue.dma_start(
                 scale_table[SCALE_ROWS[half] : SCALE_ROWS[half] + 16, :].bitcast(I32), scale_rows[8 * half : 8 * half + 8]
             )
+        iw_rows = sbuf([P, P], F32, "iw_rows")
+        for g, iw in enumerate((iw0, iw1)):
+            first_row = IW_ROW + TILES * g
+            nc.sync.dma_start(iw_rows[first_row : first_row + TILES, :], iw.rearrange("(c p) -> c p", p=P))
 
         table = sbuf([P, T], I32, "table")
         table_words = tab_words[0].rearrange("p t b -> p (t b)").bitcast(I32)
+        for lo, hi in zip(TABLE_CUTS, TABLE_CUTS[1:]):
+            nc.sync.dma_start(table[:, lo:hi], table_words[:, lo:hi])
+        w_codes = sbuf([P, 2, 2 * N], U8, "w_codes")
+        nc.sync.dma_start(w_codes[:].bitcast(I32), w_words.rearrange("a p b -> p a b").bitcast(I32))
 
-        iw_rows = placed.tile([P, P], F32, name="iw_rows", offset=T, align_bytes=ALIGN)
-        nc.gpsimd.memset(iw_rows[:], 0.0)
-        nc.scalar.dma_start(iw_rows[0:TILES, :], iw0.rearrange("(c p) -> c p", p=P))
-        nc.scalar.dma_start(iw_rows[TILES : 2 * TILES, :], iw1.rearrange("(c p) -> c p", p=P))
-        nc.scalar.dma_start(table[:, 0:SPLIT], table_words[:, 0:SPLIT])
-        zeros = sbuf([P, P], F32, "zeros")
-        nc.gpsimd.memset(zeros[:], 0.0)
+        w_planes = sbuf([P, 2 * N], U8, "w_planes")
+        nc.vector.memset(w_planes[:, 0:N].bitcast(I32), 0)
+        nc.gpsimd.memset(iw_rows[0:IW_ROW, :], 0.0)
         ident = sbuf([P, P], F32, "ident")
+        nc.gpsimd.memset(ident[:], 0.0)
         nc.gpsimd.affine_select(
             out=ident[:],
-            in_=zeros[:],
+            in_=ident[:],
             compare_op=mybir.AluOpType.not_equal,
             fill=1.0,
             base=0,
             pattern=[[-1, P]],
             channel_multiplier=1,
         )
-
-        w_planes = sbuf([P, 2 * N], U8, "w_planes")
-        nc.vector.memset(w_planes[:, 0:N].bitcast(I32), 0)
         nc.gpsimd.memset(w_planes[:, N : 2 * N].bitcast(I32), 0)
-        for r, queue in enumerate((nc.gpsimd, nc.gpsimd, nc.gpsimd, nc.sync)):
+        for r, queue in enumerate((nc.scalar, nc.gpsimd, nc.gpsimd, nc.gpsimd)):
             queue.dma_start(
                 w_planes[r:P:QUAD, :].bitcast(I32).rearrange("q (a n) -> q a n", a=2),
                 w_scales.bitcast(I32)[:, r:16:4, :].rearrange("a q n -> q a n"),
             )
 
-        nc.scalar.dma_start(table[:, SPLIT:T], table_words[:, SPLIT:T])
-        w_codes = sbuf([P, 2, 2 * N], U8, "w_codes")
-        nc.scalar.dma_start(w_codes[:].bitcast(I32), w_words.rearrange("a p b -> p a b").bitcast(I32))
-
-        iw_bank = bank([P, 2 * TILES * N], 0, "iw_bank")
+        iw_bank = bank([P, 2 * N], 4, "iw_bank")
         nc.tensor.transpose(iw_bank[:, 0:P], iw_rows[:], ident[:])
-        iw_cols = [sbuf([P, TILES], F32, "iw_cols%d" % g) for g in range(2)]
-        nc.scalar.activation(iw_cols[0][:], iw_bank[:, 0:TILES], COPY)
+        iw_cols = sbuf([P, 2 * TILES], F32, "iw_cols")
+        nc.scalar.activation(iw_cols[:], iw_bank[:, IW_ROW:P], COPY)
 
         for first_row in SCALE_ROWS:
             nc.vector.memset(scale_table[first_row - 48 : first_row, :].bitcast(I32), 0)
-
-
         picked_scales = sbuf([P, 2 * J], U8, "picked_scales")
         nc.vector.tensor_copy(picked_scales[:], scale_table[:].indirect(offsets[:]))
 
-        planes = placed.tile([P, 2, 2 * J], U8, name="planes", offset=T + LINE - 4 * J, align_bytes=LINE)
+        planes = placed.tile([P, 2, 2 * J], U8, name="planes", offset=0, align_bytes=LINE)
         for group in (0, 2, 1, 3):
             source = SCALE_ROWS[group // 2] + 8 * (group % 2)
-            nc.scalar.dma_start(
+            nc.sync.dma_start(
                 planes[QUAD * group : QUAD * group + 4, :, :].bitcast(I32),
                 picked_scales[source : source + 8, :].bitcast(I32),
             )
 
-        nc.scalar.activation(iw_cols[1][:], iw_bank[:, TILES : 2 * TILES], COPY)
-
-        wx_rows = wx.rearrange("(p t) n -> p t n", t=PACK)
-        x_rows = x.rearrange("(p t) j -> p t j", t=PACK)
-        late = placed.tile([P, PACK * (N + J)], F32, name="late", offset=T + 4 * P - ALIGN, align_bytes=ALIGN)
+        late = placed.tile([P, PACK * (N + J)], F32, name="late", offset=T - LINE, align_bytes=LINE)
         wx_raw = late[:, 0 : PACK * N].rearrange("p (t c) -> p t c", t=PACK)
-        nc.scalar.dma_start(wx_raw, wx_rows)
+        nc.sync.dma_start(wx_raw, wx.rearrange("(p t) n -> p t n", t=PACK))
+        x_rows = x.rearrange("(p t) j -> p t j", t=PACK)
         x_raw = [
             late[:, PACK * (N + HALF * h) : PACK * (N + HALF * (h + 1))].rearrange("p (t c) -> p t c", t=PACK)
             for h in range(2)
         ]
         for h in range(2):
-            nc.scalar.dma_start(x_raw[h], x_rows[:, :, HALF * h : HALF * (h + 1)])
+            nc.sync.dma_start(x_raw[h], x_rows[:, :, HALF * h : HALF * (h + 1)])
 
-        picked = sbuf([P, J + HALF], U32, "picked")
+        warm_bytes = table[:, TABLE_CUTS[1] : TABLE_CUTS[2]].bitcast(U8)
+        for index in range(2):
+            warm_up = bank([P, N], 4 + index, "warm_up%d" % index)
+            nc.tensor.matmul_mx(
+                out=warm_up[:],
+                lhsT=warm_bytes[:, 0 : 2 * P].bitcast(FP4X4),
+                lhsT_scale=picked_scales[:, 0:P],
+                rhs=warm_bytes[:, 0 : 2 * N].bitcast(FP4X4),
+                rhs_scale=picked_scales[:, 0:N],
+                start=True,
+                stop=True,
+            )
+
+        picked = sbuf([P, J], U32, "picked")
         tab_codes = {}
-        place = {(0, 0): P, (0, 1): 2 * P, (0, 2): 0, (0, 3): P}
-        place.update({(1, jt): HALF + P * jt for jt in range(TILES)})
 
-        def gather(g, lo, hi):
-            cols = slice(LIST_COLS * g + 8 * lo, LIST_COLS * g + 8 * hi)
+        def gather(g, h):
+            cols = slice(LIST_COLS * g + 16 * h, LIST_COLS * g + 16 * (h + 1))
             nc.vector.tensor_copy(
-                picked[:, place[g, lo] : place[g, lo] + P * (hi - lo)], table[:].bitcast(U32).indirect(offsets[:, cols])
+                picked[:, HALF * g : HALF * (g + 1)], table[:].bitcast(U32).indirect(offsets[:, cols])
             )
 
         def part(g, lo, hi):
             width = P * (hi - lo)
-            start = place[g, lo]
+            start = HALF * g + P * (lo % 2)
             parted = sbuf([P, 2 * 2 * width], U8, "parted%d%d" % (g, lo))
             nc.vector.tensor_copy(
                 parted[:].bitcast(U16).rearrange("p (a j) -> p a j", a=2),
@@ -149,18 +153,24 @@ def tile_list_interp_none_kernel(
                     first_byte = 2 * (a * width + P * (jt - lo))
                     tab_codes[g, a, jt] = parted[:, first_byte : first_byte + 2 * P]
 
-        gather(0, 0, 2)
+        gather(0, 0)
+        gather(1, 0)
         part(0, 0, 1)
         part(0, 1, 2)
-        gather(0, 2, 4)
-        gather(1, 0, 4)
+        part(1, 0, 2)
+        gather(0, 1)
+        gather(1, 1)
         part(0, 2, 4)
-        part(1, 0, 4)
+        part(1, 2, 4)
 
-        def project(g, jt, acc):
+        sums = {}
+        terms = {}
+
+        def project(g, jt, index):
+            sums[g, jt] = bank([P, N], index, "a%d_%d" % (g, jt))
             for a in range(2):
                 nc.tensor.matmul_mx(
-                    out=acc[:],
+                    out=sums[g, jt][:],
                     lhsT=tab_codes[g, a, jt].bitcast(FP4X4),
                     lhsT_scale=planes[:, a, g * J + P * jt : g * J + P * (jt + 1)],
                     rhs=w_codes[:, a, :].bitcast(FP4X4),
@@ -169,72 +179,78 @@ def tile_list_interp_none_kernel(
                     stop=(a == 1),
                 )
 
+        def weigh(g, jt):
+            terms[g, jt] = sbuf([P, N], F32, "term%d_%d" % (g, jt))
+            column = TILES * g + jt
+            nc.scalar.activation(terms[g, jt][:], sums[g, jt][:], COPY, scale=iw_cols[:, column : column + 1])
+
+        def weigh_and_add(jt):
+            both = sbuf([P, N], F32, "both%d" % jt)
+            column = TILES + jt
+            nc.vector.scalar_tensor_tensor(
+                both[:], sums[1, jt][:], iw_cols[:, column : column + 1], terms[0, jt][:], MULT, ADD
+            )
+            return both
+
         def interleave(copy, rows, grouped):
             copy(
                 grouped.rearrange("p (c i) t -> p c t i", i=PACK),
                 rows.rearrange("p t (c i) -> p c t i", i=PACK),
             )
-            return grouped
 
         def quantize(grouped, codes, scales, h):
             nc.vector.quantize_mx(
                 out=codes[:, HALF * h : HALF * (h + 1)].bitcast(FP8X4),
                 scales=scales[:, HALF * h : HALF * (h + 1)],
-                in_=grouped.rearrange("p c t -> p (c t)"),
+                in_=grouped[:, HALF * h : HALF * (h + 1), :].rearrange("p c t -> p (c t)"),
             )
+
+        for g, jt, index in ((0, 0, 0), (0, 1, 1), (1, 0, 2), (1, 1, 3), (0, 2, 6), (0, 3, 7)):
+            project(g, jt, index)
+            weigh(g, jt)
+        project(1, 2, 0)
+        project(1, 3, 1)
 
         wx_codes = sbuf([P, N], U32, "wx_codes")
         wx_scales = sbuf([P, N], U8, "wx_scales")
         x_codes = sbuf([P, J], U32, "x_codes")
         x_scales = sbuf([P, J], U8, "x_scales")
+        wx_grouped = sbuf([P, N * PACK], BF16, "wx_grouped")
+        wx_by_column = wx_grouped[:].rearrange("p (c t) -> p c t", t=PACK)
+        x_grouped = sbuf([P, J * PACK], BF16, "x_grouped")
+        x_by_column = x_grouped[:].rearrange("p (c t) -> p c t", t=PACK)
 
-        table_bytes = table[:, 0:SPLIT].bitcast(U8)
-        for index in range(2):
-            warm_up = bank([P, N], index, "warm_up%d" % index)
-            nc.tensor.matmul_mx(
-                out=warm_up[:],
-                lhsT=table_bytes[:, 0 : 2 * P].bitcast(FP4X4),
-                lhsT_scale=picked_scales[:, 0:P],
-                rhs=table_bytes[:, 0 : 2 * N].bitcast(FP4X4),
-                rhs_scale=picked_scales[:, 0:N],
-                start=True,
-                stop=True,
-            )
+        for h in range(2):
+            interleave(nc.vector.tensor_copy, wx_raw[:, :, HALF * h : HALF * (h + 1)], wx_by_column[:, HALF * h : HALF * (h + 1), :])
+        for h in range(2):
+            quantize(wx_by_column, wx_codes, wx_scales, h)
+        interleave(nc.scalar.copy, x_raw[0], x_by_column[:, 0:HALF, :])
+        interleave(nc.scalar.copy, x_raw[1][:, :, 0 : HALF - SHARE], x_by_column[:, HALF : J - SHARE, :])
+        to_turn = {jt: [terms[0, jt], terms[1, jt]] for jt in range(2)}
+        for jt in (2, 3):
+            to_turn[jt] = [weigh_and_add(jt)]
+        interleave(nc.vector.tensor_copy, x_raw[1][:, :, HALF - SHARE : HALF], x_by_column[:, J - SHARE : J, :])
+        for h in range(2):
+            quantize(x_by_column, x_codes, x_scales, h)
 
-        a0 = [bank([P, N], jt, "a0_%d" % jt) for jt in range(TILES)]
-        a1 = [bank([P, N], TILES + jt, "a1_%d" % jt) for jt in range(TILES)]
-        first = {}
-        both = [wx_raw[:, 0:2, 0:HALF]]
-        for jt in range(1, TILES - 1):
-            both.append(sbuf([P, 2, HALF], F32, "both%d" % jt)[:])
-        both.append(x_raw[0][:, 0:2, :])
         out_by_tile = out.rearrange("(nt p) j -> p nt j", p=P)
 
-        def weigh_first(jt):
-            first[jt] = sbuf([P, N], F32, "first%d" % jt)
-            nc.scalar.activation(first[jt][:], a0[jt][:], COPY, scale=iw_cols[0][:, jt : jt + 1])
-
-        def weigh_second(jt):
-            nc.vector.scalar_tensor_tensor(
-                both[jt],
-                a1[jt][:].rearrange("p (m c) -> p m c", m=2),
-                iw_cols[1][:, jt : jt + 1],
-                first[jt][:].rearrange("p (m c) -> p m c", m=2),
-                MULT,
-                ADD,
-            )
-
-        def finish(h):
-            turned = [bank([P, 2, HALF], 2 * h + m, "turned%d%d" % (h, m)) for m in range(2)]
-            for jt in (2 * h, 2 * h + 1):
-                for nt in range(TILES):
-                    nc.tensor.transpose(
-                        turned[nt // 2][:, nt % 2, P * (jt % 2) : P * (jt % 2 + 1)],
-                        both[jt][:, nt // 2, P * (nt % 2) : P * (nt % 2 + 1)],
-                        ident[:],
+        def finish(h, turned_banks, ax_banks):
+            turned = [bank([P, 2, HALF], turned_banks[m], "turned%d%d" % (h, m)) for m in range(2)]
+            for m in range(2):
+                steps = [(term, jt, i) for s in range(2) for jt in (2 * h, 2 * h + 1) for term in to_turn[jt][s : s + 1] for i in range(2)]
+                for step, (term, jt, i) in enumerate(steps):
+                    nt = 2 * m + i
+                    nc.tensor.matmul(
+                        turned[m][:, i, P * (jt % 2) : P * (jt % 2 + 1)],
+                        lhsT=term[:, P * nt : P * (nt + 1)],
+                        rhs=ident[:],
+                        is_transpose=True,
+                        start=(step == 0),
+                        stop=(step == len(steps) - 1),
                     )
             for m in range(2):
-                ax = bank([P, 2, HALF], TILES + 2 * h + m, "ax%d%d" % (h, m))
+                ax = bank([P, 2, HALF], ax_banks[m], "ax%d%d" % (h, m))
                 for i in range(2):
                     nt = 2 * m + i
                     nc.tensor.matmul_mx(
@@ -246,38 +262,12 @@ def tile_list_interp_none_kernel(
                         start=True,
                         stop=True,
                     )
-                cuts = (0, 1, 2)
-                for lo, hi in zip(cuts, cuts[1:]):
-                    looked_up = sbuf([P, hi - lo, HALF], F32, "looked_up%d%d%d" % (h, m, lo))
-                    nc.scalar.copy(looked_up[:], turned[m][:, lo:hi, :])
-                    result = sbuf([P, hi - lo, HALF], F32, "result%d%d%d" % (h, m, lo))
-                    nc.vector.tensor_tensor(result[:], ax[:, lo:hi, :], looked_up[:], ADD)
-                    nc.sync.dma_start(out_by_tile[:, 2 * m + lo : 2 * m + hi, HALF * h : HALF * (h + 1)], result[:])
+                for i in range(2):
+                    looked_up = sbuf([P, HALF], F32, "looked_up%d%d%d" % (h, m, i))
+                    nc.scalar.copy(looked_up[:], turned[m][:, i, :])
+                    result = sbuf([P, HALF], F32, "result%d%d%d" % (h, m, i))
+                    nc.vector.tensor_tensor(result[:], ax[:, i, :], looked_up[:], ADD)
+                    nc.sync.dma_start(out_by_tile[:, 2 * m + i, HALF * h : HALF * (h + 1)], result[:])
 
-        for jt in range(TILES):
-            project(0, jt, a0[jt])
-        for jt in range(TILES):
-            project(1, jt, a1[jt])
-
-        wx_grouped = sbuf([P, N * PACK], BF16, "wx_grouped")
-        wx_by_column = wx_grouped[:].rearrange("p (c t) -> p c t", t=PACK)
-        for jt in range(TILES):
-            weigh_first(jt)
-        interleave(nc.scalar.copy, wx_raw[:, :, N - SHARE : N], wx_by_column[:, N - SHARE : N, :])
-        for lo, hi in ((0, HALF), (HALF, N - SHARE)):
-            interleave(nc.vector.tensor_copy, wx_raw[:, :, lo:hi], wx_by_column[:, lo:hi, :])
-        quantize(wx_by_column[:, 0:HALF, :], wx_codes, wx_scales, 0)
-
-        x_grouped = sbuf([P, 2 * HALF * PACK], BF16, "x_grouped", slot="iw_cols0")
-        x_by_column = x_grouped[:].rearrange("p (c t) -> p c t", t=PACK)
-        for h in range(2):
-            interleave(nc.scalar.copy, x_raw[h], x_by_column[:, HALF * h : HALF * (h + 1), :])
-        weigh_second(0)
-        quantize(wx_by_column[:, HALF:N, :], wx_codes, wx_scales, 1)
-        weigh_second(1)
-        weigh_second(2)
-        quantize(x_by_column[:, 0:HALF, :], x_codes, x_scales, 0)
-        weigh_second(3)
-        quantize(x_by_column[:, HALF:J, :], x_codes, x_scales, 1)
-        for h in range(2):
-            finish(h)
+        finish(0, (4, 5), (2, 3))
+        finish(1, (6, 7), (0, 1))

@@ -28,7 +28,7 @@ BANK = 2048
 ALIGN = 64
 LINE = 256
 LIST_COLS = J // 16
-TABLE_CUTS = (0, T // 2, 7 * T // 8, T)
+TABLE_CUTS = (0, T // 2, 15 * T // 16, T)
 SHARE = 64
 
 
@@ -52,14 +52,14 @@ def tile_list_interp_none_kernel(
 
         scale_table = placed.tile([P, T], U8, name="scale_table", offset=0, align_bytes=LINE)
         scale_rows = tab_scales.bitcast(I32).rearrange("a q t -> q a t")
-        for half, queue in enumerate((nc.scalar, nc.scalar)):
-            queue.dma_start(
+        for half in range(2):
+            nc.sync.dma_start(
                 scale_table[SCALE_ROWS[half] : SCALE_ROWS[half] + 16, :].bitcast(I32), scale_rows[8 * half : 8 * half + 8]
             )
         iw_rows = sbuf([P, P], F32, "iw_rows")
         for g, iw in enumerate((iw0, iw1)):
             first_row = IW_ROW + TILES * g
-            nc.sync.dma_start(iw_rows[first_row : first_row + TILES, :], iw.rearrange("(c p) -> c p", p=P))
+            nc.scalar.dma_start(iw_rows[first_row : first_row + TILES, :], iw.rearrange("(c p) -> c p", p=P))
 
         table = sbuf([P, T], I32, "table")
         table_words = tab_words[0].rearrange("p t b -> p (t b)").bitcast(I32)

@@ -51,10 +51,9 @@ def tile_list_interp_none_kernel(
         nc.sync.dma_start(offsets[:], offs)
 
         scale_table = placed.tile([P, T], U8, name="scale_table", offset=0, align_bytes=LINE)
-        scale_rows = tab_scales.bitcast(I32).rearrange("a q t -> q a t")
-        for half in range(2):
-            nc.sync.dma_start(
-                scale_table[SCALE_ROWS[half] : SCALE_ROWS[half] + 16, :].bitcast(I32), scale_rows[8 * half : 8 * half + 8]
+        for a, queue in enumerate((nc.sync, nc.scalar)):
+            queue.dma_start(
+                scale_table[SCALE_ROWS[a] : SCALE_ROWS[a] + 16, :].bitcast(I32), tab_scales[a].bitcast(I32)
             )
         iw_rows = sbuf([P, P], F32, "iw_rows")
         for g, iw in enumerate((iw0, iw1)):
@@ -99,12 +98,17 @@ def tile_list_interp_none_kernel(
         picked_scales = sbuf([P, 2 * J], U8, "picked_scales")
         nc.vector.tensor_copy(picked_scales[:], scale_table[:].indirect(offsets[:]))
 
+        joined = sbuf([P, 2, 2 * J], U8, "joined")
+        for a in range(2):
+            quarter = QUAD + 2 * QUAD * a
+            nc.vector.tensor_copy(
+                joined[QUAD : 2 * QUAD, a, :].bitcast(I32), picked_scales[quarter : quarter + QUAD, :].bitcast(I32)
+            )
         planes = placed.tile([P, 2, 2 * J], U8, name="planes", offset=0, align_bytes=LINE)
-        for group in (0, 2, 1, 3):
-            source = SCALE_ROWS[group // 2] + 8 * (group % 2)
+        for r in range(4):
             nc.sync.dma_start(
-                planes[QUAD * group : QUAD * group + 4, :, :].bitcast(I32),
-                picked_scales[source : source + 8, :].bitcast(I32),
+                planes[r:P:QUAD, :, :].bitcast(I32),
+                joined[SCALE_ROWS[0] + r : SCALE_ROWS[0] + 16 : 4, :, :].bitcast(I32),
             )
 
         late = placed.tile([P, PACK * (N + J)], F32, name="late", offset=T - LINE, align_bytes=LINE)

from contextlib import ExitStack

import concourse.mybir as mybir

K, L, N, T, J = 1024, 512, 512, 4096, 512
FLOPS = 2 * (2 * K + L) * N * J

F32 = mybir.dt.float32
BF16 = mybir.dt.bfloat16
I32 = mybir.dt.int32
U32 = mybir.dt.uint32
U16 = mybir.dt.uint16
U8 = mybir.dt.uint8
FP8X4 = mybir.dt.float8_e4m3fn_x4
FP4X4 = mybir.dt.float4_e2m1fn_x4
COPY = mybir.ActivationFunctionType.Copy
MULT = mybir.AluOpType.mult
ADD = mybir.AluOpType.add

P = 128
PACK = 4
QUAD = 32
TILES = 4
HALF = 256
SCALE_ROWS = (48, 112)
IW_ROW = P - 2 * TILES
BANK = 2048
ALIGN = 64
LINE = 256
LIST_COLS = J // 16
TABLE_CUTS = (0, T // 2, 15 * T // 16, T)
SHARE = 64


def tile_list_interp_none_kernel(
    tc, tab_words, tab_scales, w_words, w_scales, x, wx, iw0, iw1, offs, out
):
    nc = tc.nc
    with ExitStack() as ctx:
        keep = ctx.enter_context(tc.tile_pool(name="keep", bufs=1))
        placed = ctx.enter_context(tc.tile_pool(name="placed", bufs=1))
        psum = ctx.enter_context(tc.psum_pool(name="psum", bufs=1))

        def sbuf(shape, dtype, name, slot=None):
            return keep.tile(shape, dtype, name=name, tag=slot or name, align_bytes=LINE)

        def bank(shape, index, name):
            return psum.tile(shape, F32, name=name, offset=BANK * index)

        offsets = keep.tile([P, 2 * LIST_COLS], U16, name="offsets")
        nc.sync.dma_start(offsets[:], offs)

        scale_table = placed.tile([P, T], U8, name="scale_table", offset=0, align_bytes=LINE)
        for a, queue in enumerate((nc.sync, nc.scalar)):
            queue.dma_start(
                scale_table[SCALE_ROWS[a] : SCALE_ROWS[a] + 16, :].bitcast(I32), tab_scales[a].bitcast(I32)
            )
        iw_rows = sbuf([P, P], F32, "iw_rows")
        for g, iw in enumerate((iw0, iw1)):
            first_row = IW_ROW + TILES * g
            nc.scalar.dma_start(iw_rows[first_row : first_row + TILES, :], iw.rearrange("(c p) -> c p", p=P))

        table = sbuf([P, T], I32, "table")
        table_words = tab_words[0].rearrange("p t b -> p (t b)").bitcast(I32)
        for lo, hi in zip(TABLE_CUTS, TABLE_CUTS[1:]):
            nc.sync.dma_start(table[:, lo:hi], table_words[:, lo:hi])
        w_codes = sbuf([P, 2, 2 * N], U8, "w_codes")
        nc.sync.dma_start(w_codes[:].bitcast(I32), w_words.rearrange("a p b -> p a b").bitcast(I32))

        w_planes = sbuf([P, 2 * N], U8, "w_planes")
        nc.vector.memset(w_planes[:, 0:N].bitcast(I32), 0)
        nc.gpsimd.memset(iw_rows[0:IW_ROW, :], 0.0)
        ident = sbuf([P, P], F32, "ident")
        nc.gpsimd.memset(ident[:], 0.0)
        nc.gpsimd.affine_select(
            out=ident[:],
            in_=ident[:],
            compare_op=mybir.AluOpType.not_equal,
            fill=1.0,
            base=0,
            pattern=[[-1, P]],
            channel_multiplier=1,
        )
        nc.gpsimd.memset(w_planes[:, N : 2 * N].bitcast(I32), 0)
        for r, queue in enumerate((nc.scalar, nc.gpsimd, nc.gpsimd, nc.gpsimd)):
            queue.dma_start(
                w_planes[r:P:QUAD, :].bitcast(I32).rearrange("q (a n) -> q a n", a=2),
                w_scales.bitcast(I32)[:, r:16:4, :].rearrange("a q n -> q a n"),
            )

        iw_bank = bank([P, 2 * N], 4, "iw_bank")
        nc.tensor.transpose(iw_bank[:, 0:P], iw_rows[:], ident[:])
        iw_cols = sbuf([P, 2 * TILES], F32, "iw_cols")
        nc.scalar.activation(iw_cols[:], iw_bank[:, IW_ROW:P], COPY)

        for first_row in SCALE_ROWS:
            nc.vector.memset(scale_table[first_row - 48 : first_row, :].bitcast(I32), 0)
        picked_scales = sbuf([P, 2 * J], U8, "picked_scales")
        nc.vector.tensor_copy(picked_scales[:], scale_table[:].indirect(offsets[:]))

        joined = sbuf([P, 2, 2 * J], U8, "joined")
        for a in range(2):
            quarter = QUAD + 2 * QUAD * a
            nc.vector.tensor_copy(
                joined[QUAD : 2 * QUAD, a, :].bitcast(I32), picked_scales[quarter : quarter + QUAD, :].bitcast(I32)
            )
        planes = placed.tile([P, 2, 2 * J], U8, name="planes", offset=0, align_bytes=LINE)
        for r in range(4):
            nc.sync.dma_start(
                planes[r:P:QUAD, :, :].bitcast(I32),
                joined[SCALE_ROWS[0] + r : SCALE_ROWS[0] + 16 : 4, :, :].bitcast(I32),
            )

        late = placed.tile([P, PACK * (N + J)], F32, name="late", offset=T - LINE, align_bytes=LINE)
        wx_raw = late[:, 0 : PACK * N].rearrange("p (t c) -> p t c", t=PACK)
        nc.sync.dma_start(wx_raw, wx.rearrange("(p t) n -> p t n", t=PACK))
        x_rows = x.rearrange("(p t) j -> p t j", t=PACK)
        x_raw = [
            late[:, PACK * (N + HALF * h) : PACK * (N + HALF * (h + 1))].rearrange("p (t c) -> p t c", t=PACK)
            for h in range(2)
        ]
        for h in range(2):
            nc.sync.dma_start(x_raw[h], x_rows[:, :, HALF * h : HALF * (h + 1)])

        warm_bytes = table[:, TABLE_CUTS[1] : TABLE_CUTS[2]].bitcast(U8)
        for index in range(2):
            warm_up = bank([P, N], 4 + index, "warm_up%d" % index)
            nc.tensor.matmul_mx(
                out=warm_up[:],
                lhsT=warm_bytes[:, 0 : 2 * P].bitcast(FP4X4),
                lhsT_scale=picked_scales[:, 0:P],
                rhs=warm_bytes[:, 0 : 2 * N].bitcast(FP4X4),
                rhs_scale=picked_scales[:, 0:N],
                start=True,
                stop=True,
            )

        picked = sbuf([P, J], U32, "picked")
        tab_codes = {}

        def gather(g, h):
            cols = slice(LIST_COLS * g + 16 * h, LIST_COLS * g + 16 * (h + 1))
            nc.vector.tensor_copy(
                picked[:, HALF * g : HALF * (g + 1)], table[:].bitcast(U32).indirect(offsets[:, cols])
            )

        def part(g, lo, hi):
            width = P * (hi - lo)
            start = HALF * g + P * (lo % 2)
            parted = sbuf([P, 2 * 2 * width], U8, "parted%d%d" % (g, lo))
            nc.vector.tensor_copy(
                parted[:].bitcast(U16).rearrange("p (a j) -> p a j", a=2),
                picked[:, start : start + width].bitcast(U16).rearrange("p (j a) -> p a j", a=2),
            )
            for jt in range(lo, hi):
                for a in range(2):
                    first_byte = 2 * (a * width + P * (jt - lo))
                    tab_codes[g, a, jt] = parted[:, first_byte : first_byte + 2 * P]

        gather(0, 0)
        gather(1, 0)
        part(0, 0, 1)
        part(0, 1, 2)
        part(1, 0, 2)
        gather(0, 1)
        gather(1, 1)
        part(0, 2, 4)
        part(1, 2, 4)

        sums = {}
        terms = {}

        def project(g, jt, index):
            sums[g, jt] = bank([P, N], index, "a%d_%d" % (g, jt))
            for a in range(2):
                nc.tensor.matmul_mx(
                    out=sums[g, jt][:],
                    lhsT=tab_codes[g, a, jt].bitcast(FP4X4),
                    lhsT_scale=planes[:, a, g * J + P * jt : g * J + P * (jt + 1)],
                    rhs=w_codes[:, a, :].bitcast(FP4X4),
                    rhs_scale=w_planes[:, a * N : (a + 1) * N],
                    start=(a == 0),
                    stop=(a == 1),
                )

        def weigh(g, jt):
            terms[g, jt] = sbuf([P, N], F32, "term%d_%d" % (g, jt))
            column = TILES * g + jt
            nc.scalar.activation(terms[g, jt][:], sums[g, jt][:], COPY, scale=iw_cols[:, column : column + 1])

        def weigh_and_add(jt):
            both = sbuf([P, N], F32, "both%d" % jt)
            column = TILES + jt
            nc.vector.scalar_tensor_tensor(
                both[:], sums[1, jt][:], iw_cols[:, column : column + 1], terms[0, jt][:], MULT, ADD
            )
            return both

        def interleave(copy, rows, grouped):
            copy(
                grouped.rearrange("p (c i) t -> p c t i", i=PACK),
                rows.rearrange("p t (c i) -> p c t i", i=PACK),
            )

        def quantize(grouped, codes, scales, h):
            nc.vector.quantize_mx(
                out=codes[:, HALF * h : HALF * (h + 1)].bitcast(FP8X4),
                scales=scales[:, HALF * h : HALF * (h + 1)],
                in_=grouped[:, HALF * h : HALF * (h + 1), :].rearrange("p c t -> p (c t)"),
            )

        for g, jt, index in ((0, 0, 0), (0, 1, 1), (1, 0, 2), (1, 1, 3), (0, 2, 6), (0, 3, 7)):
            project(g, jt, index)
            weigh(g, jt)
        project(1, 2, 0)
        project(1, 3, 1)

        wx_codes = sbuf([P, N], U32, "wx_codes")
        wx_scales = sbuf([P, N], U8, "wx_scales")
        x_codes = sbuf([P, J], U32, "x_codes")
        x_scales = sbuf([P, J], U8, "x_scales")
        wx_grouped = sbuf([P, N * PACK], BF16, "wx_grouped")
        wx_by_column = wx_grouped[:].rearrange("p (c t) -> p c t", t=PACK)
        x_grouped = sbuf([P, J * PACK], BF16, "x_grouped")
        x_by_column = x_grouped[:].rearrange("p (c t) -> p c t", t=PACK)

        for h in range(2):
            interleave(nc.vector.tensor_copy, wx_raw[:, :, HALF * h : HALF * (h + 1)], wx_by_column[:, HALF * h : HALF * (h + 1), :])
        for h in range(2):
            quantize(wx_by_column, wx_codes, wx_scales, h)
        interleave(nc.scalar.copy, x_raw[0], x_by_column[:, 0:HALF, :])
        interleave(nc.scalar.copy, x_raw[1][:, :, 0 : HALF - SHARE], x_by_column[:, HALF : J - SHARE, :])
        to_turn = {jt: [terms[0, jt], terms[1, jt]] for jt in range(2)}
        for jt in (2, 3):
            to_turn[jt] = [weigh_and_add(jt)]
        interleave(nc.vector.tensor_copy, x_raw[1][:, :, HALF - SHARE : HALF], x_by_column[:, J - SHARE : J, :])
        for h in range(2):
            quantize(x_by_column, x_codes, x_scales, h)

        out_by_tile = out.rearrange("(nt p) j -> p nt j", p=P)

        def finish(h, turned_banks, ax_banks):
            turned = [bank([P, 2, HALF], turned_banks[m], "turned%d%d" % (h, m)) for m in range(2)]
            for m in range(2):
                steps = [(term, jt, i) for s in range(2) for jt in (2 * h, 2 * h + 1) for term in to_turn[jt][s : s + 1] for i in range(2)]
                for step, (term, jt, i) in enumerate(steps):
                    nt = 2 * m + i
                    nc.tensor.matmul(
                        turned[m][:, i, P * (jt % 2) : P * (jt % 2 + 1)],
                        lhsT=term[:, P * nt : P * (nt + 1)],
                        rhs=ident[:],
                        is_transpose=True,
                        start=(step == 0),
                        stop=(step == len(steps) - 1),
                    )
            for m in range(2):
                ax = bank([P, 2, HALF], ax_banks[m], "ax%d%d" % (h, m))
                for i in range(2):
                    nt = 2 * m + i
                    nc.tensor.matmul_mx(
                        out=ax[:, i, :],
                        lhsT=wx_codes[:, P * nt : P * (nt + 1)].bitcast(FP8X4),
                        lhsT_scale=wx_scales[:, P * nt : P * (nt + 1)],
                        rhs=x_codes[:, HALF * h : HALF * (h + 1)].bitcast(FP8X4),
                        rhs_scale=x_scales[:, HALF * h : HALF * (h + 1)],
                        start=True,
                        stop=True,
                    )
                for i in range(2):
                    looked_up = sbuf([P, HALF], F32, "looked_up%d%d%d" % (h, m, i))
                    nc.scalar.copy(looked_up[:], turned[m][:, i, :])
                    result = sbuf([P, HALF], F32, "result%d%d%d" % (h, m, i))
                    nc.vector.tensor_tensor(result[:], ax[:, i, :], looked_up[:], ADD)
                    nc.sync.dma_start(out_by_tile[:, 2 * m + i, HALF * h : HALF * (h + 1)], result[:])

        finish(0, (4, 5), (2, 3))
        finish(1, (6, 7), (0, 1))
